import numpy as np
import ml_dtypes


def mxq(x, axis, fmt="e4m3"):
    dtype, down = {"e4m3": (ml_dtypes.float8_e4m3fn, 7), "e5m2": (ml_dtypes.float8_e5m2, 14)}[fmt]
    v = np.moveaxis(np.asarray(x, np.float32).astype(ml_dtypes.bfloat16).astype(np.float64), axis, -1)
    blocks = v.reshape(v.shape[:-1] + (-1, 32))
    amax = np.abs(blocks).max(-1, keepdims=True)
    byte = np.maximum(np.where(amax > 0, np.frexp(amax)[1] - 1 + 127, 0) - down, 1)
    scale = np.exp2(byte - 127.0)
    codes = (blocks / scale).astype(np.float32).astype(dtype).astype(np.float64)
    return np.moveaxis((codes * scale).reshape(v.shape), -1, axis)


WIDE = False


def mx_kscale(k):
    if not WIDE:
        return np.ones(k)
    levels = np.array([10, -10, 5, -5, 0])
    if k % 512:
        return np.exp2(np.random.permutation(np.resize(levels, k // 32))).repeat(32)
    a = np.empty((k // 512, 16))
    for p in range(k // 512):
        a[p, :8] = np.random.permutation(np.resize(levels, 8))
        for g in range(8):
            far = levels[np.abs(levels - a[p, g]) >= 10]
            a[p, g + 8] = far[np.random.randint(len(far))]
    return np.exp2(a.ravel()).repeat(32)


BF16 = ml_dtypes.bfloat16


def bf(x):
    return np.asarray(x, np.float32).astype(BF16)


def f64(x):
    return np.asarray(x).astype(np.float64)

E4M3FN = np.array([(-1.0 if i & 128 else 1.0) * ((1.0 + (i & 7) / 8.0) * 2.0 ** (((i >> 3) & 15) - 7) if i & 120 else (i & 7) * 2.0 ** -9) for i in range(256)])


def e4m3fn_bytes(y):
    return np.clip(np.asarray(y, np.float64), -448.0, 448.0).astype(np.float32).astype(ml_dtypes.float8_e4m3fn).view(np.uint8)


def e4m3fn_values(b):
    return E4M3FN[b]

def planes(Y):
    n, m = Y.shape
    b = f64(bf(Y)).reshape(n // 32, 32, m)
    amax = np.abs(b).max(1)
    byte = np.clip(np.where(amax > 0, np.frexp(amax)[1] - 1 + 127 - 7, 1), 1, 254)
    codes = (b * np.exp2(127.0 - byte)[:, None, :]).reshape(n, m).astype(np.float32).astype(ml_dtypes.float8_e4m3fn).view(np.uint8)
    words = codes.reshape(n // 512, 128, 4, m).transpose(0, 1, 3, 2)
    return np.ascontiguousarray(words), np.ascontiguousarray(byte.astype(np.uint8).reshape(n // 512, 16, m))


T, K, BLK = 2048, 1024, 128
THETA = 0.08
SPREAD = 0.8

def setup_inputs():
    s = mx_kscale(K)
    c = np.exp(SPREAD * np.random.randn(K))
    X = np.random.randn(T, K) * c[None, :] * s[None, :]
    amax = np.abs(X).reshape(T, K // BLK, BLK).max(axis=2)
    X_scale = (amax / 448.0).astype(np.float32)
    X_bytes = e4m3fn_bytes(X / np.repeat(f64(X_scale), BLK, axis=1))
    G = np.eye(K) + np.random.randn(K, K) / np.sqrt(K) * c[None, :] / c[:, None]
    B = np.random.randn(T, K) * c[None, :]
    step = 0.5 * (1.0 + 0.1 * np.random.randn(1, K))
    gain = (1.0 + 0.1 * np.random.randn(1, K)) / s[None, :]
    return {"X_bytes": X_bytes, "X_scale": X_scale, "G": bf(G / s[:, None]),
            "B": bf(B), "step": bf(step), "gain": bf(gain)}

def reference(X_bytes, X_scale, G, B, step, gain):
    X = e4m3fn_values(X_bytes) * np.repeat(f64(X_scale), BLK, axis=1)
    P = mxq(X, 1, "e4m3") @ mxq(f64(G), 0, "e4m3")
    u = X * f64(gain) - f64(step) * (P - f64(B))
    y = u - np.clip(u, -THETA, THETA)
    words, scales = planes(y.T)
    return y, words, scales

@@ -1,0 +1,347 @@
+from contextlib import ExitStack
+
+import concourse.mybir as mybir
+from concourse.masks import make_identity
+
+T, K = 2048, 1024
+THETA = 0.08
+FLOPS = 2 * T * K * K
+
+F32 = mybir.dt.float32
+BF16 = mybir.dt.bfloat16
+I32 = mybir.dt.int32
+U32 = mybir.dt.uint32
+U8 = mybir.dt.uint8
+FP8 = mybir.dt.float8_e4m3fn
+FP8X4 = mybir.dt.float8_e4m3fn_x4
+ALU = mybir.AluOpType
+ACT = mybir.ActivationFunctionType
+
+P = 128
+HALF = 512
+HALVES = K // HALF
+CHUNKS = K // P
+PAIR = 2 * P
+GROUP = 2 * PAIR
+TILES = GROUP // P
+GROUPS = T // GROUP
+STEPS = GROUPS * CHUNKS
+FRONT_LEAD = 12
+BACK_LAG = 4
+FUSED = ()
+
+
+def tile_ista_step_fp8_codes_b5_kernel(tc, X_bytes, X_scale, G, B, step, gain, out_0, out_1, out_2):
+    nc = tc.nc
+
+    with ExitStack() as ctx:
+        keep = ctx.enter_context(tc.tile_pool(name="keep", bufs=1))
+        work = ctx.enter_context(tc.tile_pool(name="work", bufs=2))
+        psum = ctx.enter_context(tc.psum_pool(name="psum", bufs=8))
+        ctx.enter_context(tc.manual_schedule())
+
+        def bank(dtype):
+            return psum.tile([P, HALF], dtype, name="bank", tag="bank")
+
+        ident_f32 = keep.tile([P, P], F32)
+        ident_bf16 = keep.tile([P, P], BF16)
+        coef_rows = keep.tile([P, P], BF16)
+        warm = keep.tile([P, 1], F32)
+        warm_out = keep.tile([P, 1], F32)
+        nc.vector.memset(coef_rows[:], 0.0)
+        nc.vector.memset(warm[:], 0.0)
+        nc.scalar.activation(out=warm_out[:], in_=warm[:], func=ACT.Relu)
+        make_identity(nc, ident_f32[:])
+        make_identity(nc, ident_bf16[:])
+
+        x_scale = keep.tile([P, T // PAIR, 2 * CHUNKS], F32)
+        x_bytes, g_raw, b_rows = {}, {}, {}
+
+        def load_x(pair):
+            x_bytes[pair] = keep.tile([P, 2 * K], U8, name="x_bytes", tag="x_bytes", bufs=T // PAIR)
+            rows = X_bytes[pair * PAIR : (pair + 1) * PAIR, :]
+            nc.sync.dma_start(out=x_bytes[pair][:], in_=rows.rearrange("(p i) k -> p (i k)", i=2))
+
+        def load_g(half, cols):
+            g_raw[half, cols] = keep.tile([P, 4, HALF], BF16, name="g_raw", tag="g_raw", bufs=4)
+            block = G[half * HALF : (half + 1) * HALF, cols * HALF : (cols + 1) * HALF]
+            nc.sync.dma_start(out=g_raw[half, cols][:], in_=block.rearrange("(p t) n -> p t n", t=4))
+
+        def load_b(group):
+            b_rows[group] = work.tile([P, 2, 2 * K], BF16, name="b_rows", tag="b_rows", bufs=3)
+            rows = B[group * GROUP : (group + 1) * GROUP, :]
+            nc.sync.dma_start(out=b_rows[group][:], in_=rows.rearrange("(q p i) n -> p q (i n)", q=2, i=2))
+
+        nc.sync.dma_start(out=x_scale[:], in_=X_scale.rearrange("(q p i) j -> p q (i j)", p=P, i=2))
+        load_x(0)
+        load_g(0, 0)
+        load_x(1)
+        load_g(1, 0)
+        nc.sync.dma_start(out=coef_rows[0:CHUNKS, :], in_=step.rearrange("o (j p) -> (o j) p", p=P))
+        nc.sync.dma_start(out=coef_rows[CHUNKS : 2 * CHUNKS, :], in_=gain.rearrange("o (j p) -> (o j) p", p=P))
+        load_b(0)
+        load_x(2)
+        load_x(3)
+        load_g(0, 1)
+        load_g(1, 1)
+        load_b(1)
+        for pair in range(4, T // PAIR):
+            load_x(pair)
+        load_b(2)
+
+        coef = keep.tile([P, 2 * CHUNKS], F32)
+        neg_step = keep.tile([P, CHUNKS], F32)
+
+        def make_coefficients():
+            turned = bank(BF16)
+            nc.tensor.transpose(turned[:, 0:P], coef_rows[:], ident_bf16[:])
+            nc.vector.tensor_copy(out=coef[:], in_=turned[:, 0 : 2 * CHUNKS])
+            nc.vector.tensor_scalar(
+                out=neg_step[:], in0=turned[:, 0:CHUNKS], scalar1=-1.0, scalar2=None, op0=ALU.mult
+            )
+
+        g_grouped, g_codes, g_scales = {}, {}, {}
+
+        def interleave_g(half, cols, copy):
+            g_grouped[half, cols] = work.tile([P, HALF, 4], BF16, name="g_grouped", tag="g_grouped", align_bytes=64)
+            copy(
+                out=g_grouped[half, cols][:].rearrange("p (c i) t -> p c t i", i=4),
+                in_=g_raw[half, cols][:].rearrange("p t (c i) -> p c t i", i=4),
+            )
+
+        def quantize_g(half, cols):
+            g_codes[half, cols] = keep.tile([P, HALF], U32, name="g_codes", tag="g_codes", bufs=4, align_bytes=64)
+            g_scales[half, cols] = keep.tile([P, HALF], U8, name="g_scales", tag="g_scales", bufs=4, align_bytes=64)
+            nc.vector.quantize_mx(
+                out=g_codes[half, cols][:].bitcast(FP8X4),
+                scales=g_scales[half, cols][:],
+                in_=g_grouped[half, cols][:].rearrange("p n t -> p (n t)"),
+            )
+
+        x32, x_sorted, x_grouped, x_codes, x_scales = {}, {}, {}, {}, {}
+
+        def widen_x(tile):
+            pair, i = divmod(tile, 2)
+            x32[tile] = work.tile([P, K], F32, name="x32", tag="x32", bufs=10)
+            for j in range(CHUNKS):
+                nc.vector.tensor_scalar(
+                    out=x32[tile][:, j * P : (j + 1) * P],
+                    in0=x_bytes[pair][:, i * K + j * P : i * K + (j + 1) * P].bitcast(FP8),
+                    scalar1=x_scale[:, pair, i * CHUNKS + j : i * CHUNKS + j + 1],
+                    scalar2=None,
+                    op0=ALU.mult,
+                )
+
+        def round_sorted(rounded, values):
+            nc.vector.tensor_copy(
+                out=rounded.rearrange("p (u w e) -> p u w e", u=2, e=2),
+                in_=values.rearrange("p (w u e) -> p u w e", u=2, e=2),
+            )
+
+        def turn_words(rounded):
+            words = rounded.bitcast(F32)
+            turned = bank(F32)
+            for a in range(2):
+                for u in range(2):
+                    nc.tensor.transpose(
+                        turned[:, (2 * a + u) * P : (2 * a + u + 1) * P],
+                        words[:, (2 * u + a) * P : (2 * u + a + 1) * P],
+                        ident_f32[:],
+                    )
+            return turned
+
+        def round_x(tile):
+            x_sorted[tile] = work.tile([P, K], BF16, name="x_sorted", tag="x_sorted")
+            round_sorted(x_sorted[tile][:], x32[tile][:])
+
+        def turn_x(tile):
+            turned = turn_words(x_sorted[tile][:])
+            x_grouped[tile] = work.tile([P, K], BF16, name="x_grouped", tag="x_grouped", align_bytes=64)
+            nc.scalar.copy(
+                out=x_grouped[tile][:].bitcast(F32).rearrange("p (h c u) -> p h c u", h=2, u=2),
+                in_=turned[:].rearrange("p (h u c) -> p h c u", h=2, u=2),
+            )
+
+        def quantize_x(tile):
+            group, i = divmod(tile, TILES)
+            if i == 0:
+                x_codes[group] = work.tile([P, HALVES, GROUP], U32, name="x_codes", tag="x_codes", align_bytes=64)
+                x_scales[group] = work.tile([P, HALVES, GROUP], U8, name="x_scales", tag="x_scales", align_bytes=64)
+            for half in range(HALVES):
+                nc.vector.quantize_mx(
+                    out=x_codes[group][:, half, i * P : (i + 1) * P].bitcast(FP8X4),
+                    scales=x_scales[group][:, half, i * P : (i + 1) * P],
+                    in_=x_grouped[tile][:, half * HALF : (half + 1) * HALF],
+                )
+
+        terms = {}
+
+        def middle(group, j):
+            cols, jj = divmod(j, TILES)
+            product = bank(F32)
+            for half in range(HALVES):
+                nc.tensor.matmul_mx(
+                    out=product[:],
+                    lhsT=g_codes[half, cols][:, jj * P : (jj + 1) * P].bitcast(FP8X4),
+                    lhsT_scale=g_scales[half, cols][:, jj * P : (jj + 1) * P],
+                    rhs=x_codes[group][:, half, :].bitcast(FP8X4),
+                    rhs_scale=x_scales[group][:, half, :],
+                    start=(half == 0),
+                    stop=(half == HALVES - 1),
+                )
+            b_turned = bank(BF16)
+            for i in range(TILES):
+                start = (i % 2) * K + j * P
+                nc.tensor.transpose(
+                    b_turned[:, i * P : (i + 1) * P], b_rows[group][:, i // 2, start : start + P], ident_bf16[:]
+                )
+            x_turned = bank(F32)
+            for i in range(TILES):
+                nc.tensor.transpose(
+                    x_turned[:, i * P : (i + 1) * P], x32[group * TILES + i][:, j * P : (j + 1) * P], ident_f32[:]
+                )
+            p_term = work.tile([P, GROUP], F32, name="p_term", tag="p_term", bufs=3)
+            nc.scalar.activation(out=p_term[:], in_=product[:], func=ACT.Copy, scale=neg_step[:, j : j + 1])
+            px_term = work.tile([P, GROUP], F32, name="px_term", tag="px_term", bufs=10)
+            b_term = work.tile([P, GROUP], F32, name="b_term", tag="b_term", bufs=10)
+            if j not in FUSED:
+                nc.scalar.activation(out=b_term[:], in_=b_turned[:], func=ACT.Copy, scale=coef[:, j : j + 1])
+            nc.vector.scalar_tensor_tensor(
+                out=px_term[:],
+                in0=x_turned[:],
+                scalar=coef[:, CHUNKS + j : CHUNKS + j + 1],
+                in1=p_term[:],
+                op0=ALU.mult,
+                op1=ALU.add,
+            )
+            if j in FUSED:
+                nc.vector.scalar_tensor_tensor(
+                    out=b_term[:],
+                    in0=b_turned[:],
+                    scalar=coef[:, j : j + 1],
+                    in1=px_term[:],
+                    op0=ALU.mult,
+                    op1=ALU.add,
+                )
+                terms[group, j] = [b_term]
+            else:
+                terms[group, j] = [px_term, b_term]
+
+        u_bank, above, y_rows, y_sorted, y_grouped, y_scales = {}, {}, {}, {}, {}, {}
+
+        def back_item(m):
+            group, rest = divmod(m, CHUNKS)
+            half, i = divmod(rest, TILES)
+            return group, half, i
+
+        def turn_back(m):
+            group, half, i = back_item(m)
+            u_bank[m] = bank(F32)
+            for jj in range(TILES):
+                addends = terms[group, half * TILES + jj]
+                for a, term in enumerate(addends):
+                    nc.tensor.matmul(
+                        out=u_bank[m][:, jj * P : (jj + 1) * P],
+                        lhsT=term[:, i * P : (i + 1) * P],
+                        rhs=ident_f32[:],
+                        is_transpose=True,
+                        start=(a == 0),
+                        stop=(a == len(addends) - 1),
+                    )
+            above[m] = work.tile([P, HALF], F32, name="above", tag="above")
+            nc.scalar.activation(out=above[m][:], in_=u_bank[m][:], func=ACT.Relu, bias=-THETA)
+
+        def threshold(m):
+            group, half, i = back_item(m)
+            if i % 2 == 0:
+                y_rows[m // 2] = work.tile([P, 2, HALF], F32, name="y_rows", tag="y_rows", bufs=3)
+            nc.vector.scalar_tensor_tensor(
+                out=y_rows[m // 2][:, i % 2, :],
+                in0=u_bank[m][:],
+                scalar=THETA,
+                in1=above[m][:],
+                op0=ALU.add,
+                op1=ALU.min,
+            )
+            if i % 2 == 1:
+                first = group * GROUP + (i // 2) * PAIR
+                rows = out_0[first : first + PAIR, half * HALF : (half + 1) * HALF]
+                nc.sync.dma_start(out=rows.rearrange("(p i) n -> p i n", i=2), in_=y_rows[m // 2][:])
+
+        def round_y(mp):
+            y_sorted[mp] = work.tile([P, K], BF16, name="y_sorted", tag="y_sorted")
+            round_sorted(y_sorted[mp][:], y_rows[mp][:].rearrange("p i n -> p (i n)"))
+
+        def turn_y(mp):
+            turned = turn_words(y_sorted[mp][:])
+            y_grouped[mp] = work.tile([P, K], BF16, name="y_grouped", tag="y_grouped", align_bytes=64)
+            nc.scalar.copy(
+                out=y_grouped[mp][:].bitcast(F32).rearrange("p (c a) -> p c a", a=4),
+                in_=turned[:].rearrange("p (a c) -> p c a", a=4),
+            )
+
+        def quantize_y(mp):
+            group, half, i = back_item(2 * mp)
+            q = i // 2
+            if half == 0 and q == 0:
+                y_scales[group] = work.tile([P, HALVES, GROUP], U8, name="y_scales", tag="y_scales", align_bytes=64)
+            y_codes = work.tile([P, PAIR], U32, name="y_codes", tag="y_codes", bufs=3, align_bytes=64)
+            nc.vector.quantize_mx(
+                out=y_codes[:].bitcast(FP8X4),
+                scales=y_scales[group][:, half, q * PAIR : (q + 1) * PAIR],
+                in_=y_grouped[mp][:],
+            )
+            first = group * GROUP + q * PAIR
+            words = out_1[half, :, first : first + PAIR, :].rearrange("p m t -> p (m t)")
+            nc.sync.dma_start(out=words.bitcast(I32), in_=y_codes[:].bitcast(I32))
+            if half == HALVES - 1 and q == 1:
+                planes = out_2[:, :, group * GROUP : (group + 1) * GROUP].bitcast(I32)
+                for quadrant in range(4):
+                    nc.sync.dma_start(
+                        out=planes[:, 4 * quadrant : 4 * quadrant + 4, :].rearrange("h r m -> r h m"),
+                        in_=y_scales[group][32 * quadrant : 32 * quadrant + 4, :, :].bitcast(I32),
+                    )
+
+        tiles = range(T // P)
+        items = range(STEPS)
+        pairs = range(STEPS // 2)
+        for n in range(-FRONT_LEAD, STEPS + BACK_LAG + 5):
+            s = n + FRONT_LEAD
+            m = n - BACK_LAG
+            if n == -FRONT_LEAD + 1:
+                interleave_g(0, 0, nc.scalar.copy)
+            if n == -FRONT_LEAD + 5:
+                interleave_g(1, 0, nc.scalar.copy)
+            if n == -FRONT_LEAD + 6:
+                quantize_g(0, 0)
+                make_coefficients()
+            if n == -3:
+                quantize_g(1, 0)
+            if n in (-2, 0):
+                interleave_g(n // 2 + 1, 1, nc.vector.tensor_copy)
+            if n in items:
+                middle(*divmod(n, CHUNKS))
+            if n in (-1, 1):
+                quantize_g((n + 1) // 2, 1)
+            if n == CHUNKS:
+                load_b(3)
+            if m in items:
+                turn_back(m)
+            if n % 2 == 0:
+                if s // 2 - 1 in tiles:
+                    turn_x(s // 2 - 1)
+                if m // 2 - 1 in pairs:
+                    round_y(m // 2 - 1)
+                if s // 2 in tiles:
+                    widen_x(s // 2)
+            else:
+                if m // 2 - 1 in pairs:
+                    turn_y(m // 2 - 1)
+                if s // 2 - 1 in tiles:
+                    quantize_x(s // 2 - 1)
+                if m // 2 - 2 in pairs:
+                    quantize_y(m // 2 - 2)
+                if s // 2 in tiles:
+                    round_x(s // 2)
+            if m in items:
+                threshold(m)

@@ -22,13 +22,45 @@ HALF = 512
 HALVES = K // HALF
 CHUNKS = K // P
 PAIR = 2 * P
-GROUP = 2 * PAIR
-TILES = GROUP // P
-GROUPS = T // GROUP
-STEPS = GROUPS * CHUNKS
-FRONT_LEAD = 12
-BACK_LAG = 4
-FUSED = ()
+PAIRS = T // PAIR
+QUARTER = 2 * P
+STEPS = 4 * PAIRS
+GROUP_PAIRS = (1,) * 8
+B_BUFS = 5
+X32_BUFS = 8
+XC_BUFS = 3
+TERM_BUFS = 7
+SCALE_PAIRS = 2
+Y_LAG = 0
+MX_PAIRED = False
+
+
+def front_step(tile):
+    return 2*tile-8 if tile>3 else tile-3
+
+
+def g_step(half, c):
+    return c-2
+
+
+def g_on_scalar(half, c):
+    return half==1
+
+
+def widen_on_scalar(tile, j):
+    return tile==1
+
+
+def round_x_engine(tile):
+    return "vector"
+
+
+def round_y_engine(mp):
+    return "vector"
+
+
+def fused(n):
+    return False
 
 
 def tile_ista_step_fp8_codes_b5_kernel(tc, X_bytes, X_scale, G, B, step, gain, out_0, out_1, out_2):
@@ -38,7 +70,7 @@ def tile_ista_step_fp8_codes_b5_kernel(tc, X_bytes, X_scale, G, B, step, gain, o
         keep = ctx.enter_context(tc.tile_pool(name="keep", bufs=1))
         work = ctx.enter_context(tc.tile_pool(name="work", bufs=2))
         psum = ctx.enter_context(tc.psum_pool(name="psum", bufs=8))
-        ctx.enter_context(tc.manual_schedule())
+        ctx.enter_context(tc.manual_schedule(engines={mybir.EngineType.PE, mybir.EngineType.SP}))
 
         def bank(dtype):
             return psum.tile([P, HALF], dtype, name="bank", tag="bank")
@@ -54,7 +86,8 @@ def tile_ista_step_fp8_codes_b5_kernel(tc, X_bytes, X_scale, G, B, step, gain, o
         make_identity(nc, ident_f32[:])
         make_identity(nc, ident_bf16[:])
 
-        x_scale = keep.tile([P, T // PAIR, 2 * CHUNKS], F32)
+        first_scale = keep.tile([P, 2 * CHUNKS], F32)
+        x_scale = keep.tile([P, PAIRS - 1, 2 * CHUNKS], F32)
         x_bytes, g_raw, b_rows = {}, {}, {}
 
         def load_x(pair):
@@ -62,32 +95,41 @@ def tile_ista_step_fp8_codes_b5_kernel(tc, X_bytes, X_scale, G, B, step, gain, o
             rows = X_bytes[pair * PAIR : (pair + 1) * PAIR, :]
             nc.sync.dma_start(out=x_bytes[pair][:], in_=rows.rearrange("(p i) k -> p (i k)", i=2))
 
-        def load_g(half, cols):
-            g_raw[half, cols] = keep.tile([P, 4, HALF], BF16, name="g_raw", tag="g_raw", bufs=4)
-            block = G[half * HALF : (half + 1) * HALF, cols * HALF : (cols + 1) * HALF]
-            nc.sync.dma_start(out=g_raw[half, cols][:], in_=block.rearrange("(p t) n -> p t n", t=4))
+        def load_g(half, first, last):
+            width = (last - first) * QUARTER
+            raw = keep.tile([P, 4, width], BF16, name="g_raw", tag="g_raw%d_%d" % (half, first))
+            block = G[half * HALF : (half + 1) * HALF, first * QUARTER : last * QUARTER]
+            nc.sync.dma_start(out=raw[:], in_=block.rearrange("(p t) n -> p t n", t=4))
+            for c in range(first, last):
+                g_raw[half, c] = raw[:, :, (c - first) * QUARTER : (c - first + 1) * QUARTER]
 
-        def load_b(group):
-            b_rows[group] = work.tile([P, 2, 2 * K], BF16, name="b_rows", tag="b_rows", bufs=3)
-            rows = B[group * GROUP : (group + 1) * GROUP, :]
-            nc.sync.dma_start(out=b_rows[group][:], in_=rows.rearrange("(q p i) n -> p q (i n)", q=2, i=2))
+        def load_b(pair):
+            b_rows[pair] = work.tile([P, 2 * K], BF16, name="b_rows", tag="b_rows", bufs=B_BUFS)
+            rows = B[pair * PAIR : (pair + 1) * PAIR, :]
+            nc.sync.dma_start(out=b_rows[pair][:], in_=rows.rearrange("(p i) n -> p (i n)", i=2))
 
-        nc.sync.dma_start(out=x_scale[:], in_=X_scale.rearrange("(q p i) j -> p q (i j)", p=P, i=2))
+        scale_rows = X_scale.rearrange("(q p i) j -> p q (i j)", p=P, i=2)
         load_x(0)
-        load_g(0, 0)
-        load_x(1)
-        load_g(1, 0)
+        nc.sync.dma_start(out=first_scale[:], in_=scale_rows[:, 0, :])
+        load_g(0, 0, 1)
+        load_g(1, 0, 1)
         nc.sync.dma_start(out=coef_rows[0:CHUNKS, :], in_=step.rearrange("o (j p) -> (o j) p", p=P))
         nc.sync.dma_start(out=coef_rows[CHUNKS : 2 * CHUNKS, :], in_=gain.rearrange("o (j p) -> (o j) p", p=P))
         load_b(0)
+        load_g(0, 1, 2)
+        load_g(1, 1, 2)
+        load_x(1)
+        nc.sync.dma_start(out=x_scale[:], in_=scale_rows[:, 1:, :])
+        load_g(0, 2, 4)
+        load_g(1, 2, 4)
         load_x(2)
-        load_x(3)
-        load_g(0, 1)
-        load_g(1, 1)
         load_b(1)
-        for pair in range(4, T // PAIR):
-            load_x(pair)
+        load_x(3)
         load_b(2)
+        for pair in range(4, PAIRS):
+            load_x(pair)
+        for pair in range(3, B_BUFS):
+            load_b(pair)
 
         coef = keep.tile([P, 2 * CHUNKS], F32)
         neg_step = keep.tile([P, CHUNKS], F32)
@@ -102,41 +144,51 @@ def tile_ista_step_fp8_codes_b5_kernel(tc, X_bytes, X_scale, G, B, step, gain, o
 
         g_grouped, g_codes, g_scales = {}, {}, {}
 
-        def interleave_g(half, cols, copy):
-            g_grouped[half, cols] = work.tile([P, HALF, 4], BF16, name="g_grouped", tag="g_grouped", align_bytes=64)
+        def interleave_g(half, c, copy):
+            g_grouped[half, c] = work.tile([P, QUARTER, 4], BF16, name="g_grouped", tag="g_grouped", bufs=4, align_bytes=64)
             copy(
-                out=g_grouped[half, cols][:].rearrange("p (c i) t -> p c t i", i=4),
-                in_=g_raw[half, cols][:].rearrange("p t (c i) -> p c t i", i=4),
+                out=g_grouped[half, c][:].rearrange("p (c i) t -> p c t i", i=4),
+                in_=g_raw[half, c].rearrange("p t (c i) -> p c t i", i=4),
             )
 
-        def quantize_g(half, cols):
-            g_codes[half, cols] = keep.tile([P, HALF], U32, name="g_codes", tag="g_codes", bufs=4, align_bytes=64)
-            g_scales[half, cols] = keep.tile([P, HALF], U8, name="g_scales", tag="g_scales", bufs=4, align_bytes=64)
+        def quantize_g(half, c):
+            g_codes[half, c] = keep.tile([P, QUARTER], U32, name="g_codes", tag="g_codes", bufs=8, align_bytes=64)
+            g_scales[half, c] = keep.tile([P, QUARTER], U8, name="g_scales", tag="g_scales", bufs=8, align_bytes=64)
             nc.vector.quantize_mx(
-                out=g_codes[half, cols][:].bitcast(FP8X4),
-                scales=g_scales[half, cols][:],
-                in_=g_grouped[half, cols][:].rearrange("p n t -> p (n t)"),
+                out=g_codes[half, c][:].bitcast(FP8X4),
+                scales=g_scales[half, c][:],
+                in_=g_grouped[half, c][:].rearrange("p n t -> p (n t)"),
             )
+
+        group_of, first_pair = [], []
+        for group, size in enumerate(GROUP_PAIRS):
+            first_pair.append(len(group_of))
+            group_of.extend([group] * size)
 
         x32, x_sorted, x_grouped, x_codes, x_scales = {}, {}, {}, {}, {}
 
         def widen_x(tile):
             pair, i = divmod(tile, 2)
-            x32[tile] = work.tile([P, K], F32, name="x32", tag="x32", bufs=10)
+            scales = first_scale[:] if pair == 0 else x_scale[:, pair - 1, :]
+            x32[tile] = work.tile([P, K], F32, name="x32", tag="x32", bufs=X32_BUFS)
             for j in range(CHUNKS):
-                nc.vector.tensor_scalar(
-                    out=x32[tile][:, j * P : (j + 1) * P],
-                    in0=x_bytes[pair][:, i * K + j * P : i * K + (j + 1) * P].bitcast(FP8),
-                    scalar1=x_scale[:, pair, i * CHUNKS + j : i * CHUNKS + j + 1],
-                    scalar2=None,
-                    op0=ALU.mult,
-                )
+                values = x32[tile][:, j * P : (j + 1) * P]
+                codes = x_bytes[pair][:, i * K + j * P : i * K + (j + 1) * P].bitcast(FP8)
+                scale = scales[:, i * CHUNKS + j : i * CHUNKS + j + 1]
+                if widen_on_scalar(tile, j):
+                    nc.scalar.activation(out=values, in_=codes, func=ACT.Copy, scale=scale)
+                else:
+                    nc.vector.tensor_scalar(out=values, in0=codes, scalar1=scale, scalar2=None, op0=ALU.mult)
 
-        def round_sorted(rounded, values):
-            nc.vector.tensor_copy(
-                out=rounded.rearrange("p (u w e) -> p u w e", u=2, e=2),
-                in_=values.rearrange("p (w u e) -> p u w e", u=2, e=2),
-            )
+        def round_sorted(rounded, values, engine):
+            rounded = rounded.rearrange("p (u w e) -> p u w e", u=2, e=2)
+            values = values.rearrange("p (w u e) -> p u w e", u=2, e=2)
+            if engine == "gpsimd":
+                nc.gpsimd.tensor_scalar(out=rounded, in0=values, scalar1=1.0, scalar2=1.0, op0=ALU.mult, op1=ALU.mult)
+            elif engine == "scalar":
+                nc.scalar.copy(out=rounded, in_=values)
+            else:
+                nc.vector.tensor_copy(out=rounded, in_=values)
 
         def turn_words(rounded):
             words = rounded.bitcast(F32)
@@ -152,7 +204,7 @@ def tile_ista_step_fp8_codes_b5_kernel(tc, X_bytes, X_scale, G, B, step, gain, o
 
         def round_x(tile):
             x_sorted[tile] = work.tile([P, K], BF16, name="x_sorted", tag="x_sorted")
-            round_sorted(x_sorted[tile][:], x32[tile][:])
+            round_sorted(x_sorted[tile][:], x32[tile][:], round_x_engine(tile))
 
         def turn_x(tile):
             turned = turn_words(x_sorted[tile][:])
@@ -163,10 +215,12 @@ def tile_ista_step_fp8_codes_b5_kernel(tc, X_bytes, X_scale, G, B, step, gain, o
             )
 
         def quantize_x(tile):
-            group, i = divmod(tile, TILES)
+            group = group_of[tile // 2]
+            i = tile - 2 * first_pair[group]
+            width = GROUP_PAIRS[group] * PAIR
             if i == 0:
-                x_codes[group] = work.tile([P, HALVES, GROUP], U32, name="x_codes", tag="x_codes", align_bytes=64)
-                x_scales[group] = work.tile([P, HALVES, GROUP], U8, name="x_scales", tag="x_scales", align_bytes=64)
+                x_codes[group] = work.tile([P, HALVES, width], U32, name="x_codes", tag="x_codes", bufs=XC_BUFS, align_bytes=64)
+                x_scales[group] = work.tile([P, HALVES, width], U8, name="x_scales", tag="x_scales", bufs=XC_BUFS, align_bytes=64)
             for half in range(HALVES):
                 nc.vector.quantize_mx(
                     out=x_codes[group][:, half, i * P : (i + 1) * P].bitcast(FP8X4),
@@ -174,71 +228,94 @@ def tile_ista_step_fp8_codes_b5_kernel(tc, X_bytes, X_scale, G, B, step, gain, o
                     in_=x_grouped[tile][:, half * HALF : (half + 1) * HALF],
                 )
 
-        terms = {}
+        terms, products = {}, {}
 
-        def middle(group, j):
-            cols, jj = divmod(j, TILES)
-            product = bank(F32)
-            for half in range(HALVES):
-                nc.tensor.matmul_mx(
-                    out=product[:],
-                    lhsT=g_codes[half, cols][:, jj * P : (jj + 1) * P].bitcast(FP8X4),
-                    lhsT_scale=g_scales[half, cols][:, jj * P : (jj + 1) * P],
-                    rhs=x_codes[group][:, half, :].bitcast(FP8X4),
-                    rhs_scale=x_scales[group][:, half, :],
-                    start=(half == 0),
-                    stop=(half == HALVES - 1),
-                )
+        def chunks_of(n):
+            group = group_of[n // 4]
+            size = GROUP_PAIRS[group]
+            count = 2 // size
+            first = (n - 4 * first_pair[group]) * count
+            return group, size * PAIR, range(first, first + count)
+
+        def multiply(n):
+            group, width, chunks = chunks_of(n)
+            products[n] = bank(F32)
+            for slot, j in enumerate(chunks):
+                c, jj = divmod(j, 2)
+                for half in range(HALVES):
+                    nc.tensor.matmul_mx(
+                        out=products[n][:, slot * width : (slot + 1) * width],
+                        lhsT=g_codes[half, c][:, jj * P : (jj + 1) * P].bitcast(FP8X4),
+                        lhsT_scale=g_scales[half, c][:, jj * P : (jj + 1) * P],
+                        rhs=x_codes[group][:, half, :].bitcast(FP8X4),
+                        rhs_scale=x_scales[group][:, half, :],
+                        start=(half == 0),
+                        stop=(half == HALVES - 1),
+                    )
+
+        def middle(n):
+            group, width, chunks = chunks_of(n)
+            group_tiles = range(2 * first_pair[group], 2 * first_pair[group] + width // P)
             b_turned = bank(BF16)
-            for i in range(TILES):
-                start = (i % 2) * K + j * P
-                nc.tensor.transpose(
-                    b_turned[:, i * P : (i + 1) * P], b_rows[group][:, i // 2, start : start + P], ident_bf16[:]
-                )
             x_turned = bank(F32)
-            for i in range(TILES):
-                nc.tensor.transpose(
-                    x_turned[:, i * P : (i + 1) * P], x32[group * TILES + i][:, j * P : (j + 1) * P], ident_f32[:]
+            for slot, j in enumerate(chunks):
+                for i, tile in enumerate(group_tiles):
+                    start = (tile % 2) * K + j * P
+                    cols = slice(slot * width + i * P, slot * width + (i + 1) * P)
+                    nc.tensor.transpose(b_turned[:, cols], b_rows[tile // 2][:, start : start + P], ident_bf16[:])
+            for slot, j in enumerate(chunks):
+                for i, tile in enumerate(group_tiles):
+                    cols = slice(slot * width + i * P, slot * width + (i + 1) * P)
+                    nc.tensor.transpose(x_turned[:, cols], x32[tile][:, j * P : (j + 1) * P], ident_f32[:])
+            p_term = work.tile([P, HALF], F32, name="p_term", tag="p_term", bufs=3)
+            px_term = work.tile([P, HALF], F32, name="px_term", tag="px_term", bufs=TERM_BUFS)
+            b_term = work.tile([P, HALF], F32, name="b_term", tag="b_term", bufs=TERM_BUFS)
+            spans = [(slice(slot * width, (slot + 1) * width), j) for slot, j in enumerate(chunks)]
+            for cols, j in spans:
+                nc.scalar.activation(
+                    out=p_term[:, cols], in_=products[n][:, cols], func=ACT.Copy, scale=neg_step[:, j : j + 1]
                 )
-            p_term = work.tile([P, GROUP], F32, name="p_term", tag="p_term", bufs=3)
-            nc.scalar.activation(out=p_term[:], in_=product[:], func=ACT.Copy, scale=neg_step[:, j : j + 1])
-            px_term = work.tile([P, GROUP], F32, name="px_term", tag="px_term", bufs=10)
-            b_term = work.tile([P, GROUP], F32, name="b_term", tag="b_term", bufs=10)
-            if j not in FUSED:
-                nc.scalar.activation(out=b_term[:], in_=b_turned[:], func=ACT.Copy, scale=coef[:, j : j + 1])
-            nc.vector.scalar_tensor_tensor(
-                out=px_term[:],
-                in0=x_turned[:],
-                scalar=coef[:, CHUNKS + j : CHUNKS + j + 1],
-                in1=p_term[:],
-                op0=ALU.mult,
-                op1=ALU.add,
-            )
-            if j in FUSED:
+            if not fused(n):
+                for cols, j in spans:
+                    nc.scalar.activation(
+                        out=b_term[:, cols], in_=b_turned[:, cols], func=ACT.Copy, scale=coef[:, j : j + 1]
+                    )
+            for cols, j in spans:
                 nc.vector.scalar_tensor_tensor(
-                    out=b_term[:],
-                    in0=b_turned[:],
-                    scalar=coef[:, j : j + 1],
-                    in1=px_term[:],
+                    out=px_term[:, cols],
+                    in0=x_turned[:, cols],
+                    scalar=coef[:, CHUNKS + j : CHUNKS + j + 1],
+                    in1=p_term[:, cols],
                     op0=ALU.mult,
                     op1=ALU.add,
                 )
-                terms[group, j] = [b_term]
-            else:
-                terms[group, j] = [px_term, b_term]
+            for cols, j in spans:
+                if fused(n):
+                    nc.vector.scalar_tensor_tensor(
+                        out=b_term[:, cols],
+                        in0=b_turned[:, cols],
+                        scalar=coef[:, j : j + 1],
+                        in1=px_term[:, cols],
+                        op0=ALU.mult,
+                        op1=ALU.add,
+                    )
+                    terms[group, j] = [b_term[:, cols]]
+                else:
+                    terms[group, j] = [px_term[:, cols], b_term[:, cols]]
 
         u_bank, above, y_rows, y_sorted, y_grouped, y_scales = {}, {}, {}, {}, {}, {}
 
-        def back_item(m):
-            group, rest = divmod(m, CHUNKS)
-            half, i = divmod(rest, TILES)
-            return group, half, i
+        back_items = []
+        for group, size in enumerate(GROUP_PAIRS):
+            for half in range(HALVES):
+                for i in range(2 * size):
+                    back_items.append((group, half, i))
 
         def turn_back(m):
-            group, half, i = back_item(m)
+            group, half, i = back_items[m]
             u_bank[m] = bank(F32)
-            for jj in range(TILES):
-                addends = terms[group, half * TILES + jj]
+            for jj in range(4):
+                addends = terms[group, half * 4 + jj]
                 for a, term in enumerate(addends):
                     nc.tensor.matmul(
                         out=u_bank[m][:, jj * P : (jj + 1) * P],
@@ -248,11 +325,11 @@ def tile_ista_step_fp8_codes_b5_kernel(tc, X_bytes, X_scale, G, B, step, gain, o
                         start=(a == 0),
                         stop=(a == len(addends) - 1),
                     )
-            above[m] = work.tile([P, HALF], F32, name="above", tag="above")
+            above[m] = work.tile([P, HALF], F32, name="above", tag="above", bufs=3)
             nc.scalar.activation(out=above[m][:], in_=u_bank[m][:], func=ACT.Relu, bias=-THETA)
 
         def threshold(m):
-            group, half, i = back_item(m)
+            group, half, i = back_items[m]
             if i % 2 == 0:
                 y_rows[m // 2] = work.tile([P, 2, HALF], F32, name="y_rows", tag="y_rows", bufs=3)
             nc.vector.scalar_tensor_tensor(
@@ -264,13 +341,13 @@ def tile_ista_step_fp8_codes_b5_kernel(tc, X_bytes, X_scale, G, B, step, gain, o
                 op1=ALU.min,
             )
             if i % 2 == 1:
-                first = group * GROUP + (i // 2) * PAIR
+                first = (first_pair[group] + i // 2) * PAIR
                 rows = out_0[first : first + PAIR, half * HALF : (half + 1) * HALF]
                 nc.sync.dma_start(out=rows.rearrange("(p i) n -> p i n", i=2), in_=y_rows[m // 2][:])
 
         def round_y(mp):
             y_sorted[mp] = work.tile([P, K], BF16, name="y_sorted", tag="y_sorted")
-            round_sorted(y_sorted[mp][:], y_rows[mp][:].rearrange("p i n -> p (i n)"))
+            round_sorted(y_sorted[mp][:], y_rows[mp][:].rearrange("p i n -> p (i n)"), round_y_engine(mp))
 
         def turn_y(mp):
             turned = turn_words(y_sorted[mp][:])
@@ -281,67 +358,78 @@ def tile_ista_step_fp8_codes_b5_kernel(tc, X_bytes, X_scale, G, B, step, gain, o
             )
 
         def quantize_y(mp):
-            group, half, i = back_item(2 * mp)
-            q = i // 2
-            if half == 0 and q == 0:
-                y_scales[group] = work.tile([P, HALVES, GROUP], U8, name="y_scales", tag="y_scales", align_bytes=64)
+            group, half, i = back_items[2 * mp]
+            pair = first_pair[group] + i // 2
+            store, q = divmod(pair, SCALE_PAIRS)
+            if store not in y_scales:
+                y_scales[store] = work.tile([P, HALVES, SCALE_PAIRS * PAIR], U8, name="y_scales", tag="y_scales", align_bytes=64)
             y_codes = work.tile([P, PAIR], U32, name="y_codes", tag="y_codes", bufs=3, align_bytes=64)
             nc.vector.quantize_mx(
                 out=y_codes[:].bitcast(FP8X4),
-                scales=y_scales[group][:, half, q * PAIR : (q + 1) * PAIR],
+                scales=y_scales[store][:, half, q * PAIR : (q + 1) * PAIR],
                 in_=y_grouped[mp][:],
             )
-            first = group * GROUP + q * PAIR
+            first = pair * PAIR
             words = out_1[half, :, first : first + PAIR, :].rearrange("p m t -> p (m t)")
             nc.sync.dma_start(out=words.bitcast(I32), in_=y_codes[:].bitcast(I32))
-            if half == HALVES - 1 and q == 1:
-                planes = out_2[:, :, group * GROUP : (group + 1) * GROUP].bitcast(I32)
+            if half == HALVES - 1 and q == SCALE_PAIRS - 1:
+                planes = out_2[:, :, store * SCALE_PAIRS * PAIR : (store + 1) * SCALE_PAIRS * PAIR].bitcast(I32)
                 for quadrant in range(4):
                     nc.sync.dma_start(
                         out=planes[:, 4 * quadrant : 4 * quadrant + 4, :].rearrange("h r m -> r h m"),
-                        in_=y_scales[group][32 * quadrant : 32 * quadrant + 4, :, :].bitcast(I32),
+                        in_=y_scales[store][32 * quadrant : 32 * quadrant + 4, :, :].bitcast(I32),
                     )
 
-        tiles = range(T // P)
-        items = range(STEPS)
-        pairs = range(STEPS // 2)
-        for n in range(-FRONT_LEAD, STEPS + BACK_LAG + 5):
-            s = n + FRONT_LEAD
-            m = n - BACK_LAG
-            if n == -FRONT_LEAD + 1:
-                interleave_g(0, 0, nc.scalar.copy)
-            if n == -FRONT_LEAD + 5:
-                interleave_g(1, 0, nc.scalar.copy)
-            if n == -FRONT_LEAD + 6:
-                quantize_g(0, 0)
-                make_coefficients()
-            if n == -3:
-                quantize_g(1, 0)
-            if n in (-2, 0):
-                interleave_g(n // 2 + 1, 1, nc.vector.tensor_copy)
-            if n in items:
-                middle(*divmod(n, CHUNKS))
-            if n in (-1, 1):
-                quantize_g((n + 1) // 2, 1)
-            if n == CHUNKS:
-                load_b(3)
-            if m in items:
-                turn_back(m)
-            if n % 2 == 0:
-                if s // 2 - 1 in tiles:
-                    turn_x(s // 2 - 1)
-                if m // 2 - 1 in pairs:
-                    round_y(m // 2 - 1)
-                if s // 2 in tiles:
-                    widen_x(s // 2)
-            else:
-                if m // 2 - 1 in pairs:
-                    turn_y(m // 2 - 1)
-                if s // 2 - 1 in tiles:
-                    quantize_x(s // 2 - 1)
-                if m // 2 - 2 in pairs:
-                    quantize_y(m // 2 - 2)
-                if s // 2 in tiles:
-                    round_x(s // 2)
-            if m in items:
-                threshold(m)
+        RX_PHASE, BACK_LAG, BACK_PHASE, Y_PHASE = 4, 0, 1, 6
+        plan = {}
+
+        def at(n, phase, fn, *args):
+            plan.setdefault((n, phase), []).append((fn, args))
+
+        widen_x(0)
+        widen_x(1)
+        interleave_g(0, 0, nc.vector.tensor_copy)
+        interleave_g(1, 0, nc.scalar.copy)
+        round_x(0)
+        round_x(1)
+        turn_x(0)
+        turn_x(1)
+        make_coefficients()
+        quantize_g(0, 0)
+        quantize_g(1, 0)
+        interleave_g(0, 1, nc.vector.tensor_copy)
+        interleave_g(1, 1, nc.scalar.copy)
+        quantize_x(0)
+        quantize_x(1)
+        quantize_g(0, 1)
+        for tile in range(2, 2 * PAIRS):
+            n = front_step(tile)
+            at(n, 5, widen_x, tile)
+            at(n + 1, RX_PHASE if round_x_engine(tile) != "gpsimd" else -1, round_x, tile)
+            at(n + 2, 2, turn_x, tile)
+            at(n + 3, 3, quantize_x, tile)
+        at(-1, 9, quantize_g, 1, 1)
+        for c in range(2, 4):
+            for half in range(HALVES):
+                n = g_step(half, c)
+                at(n, 4, interleave_g, half, c, nc.scalar.copy if g_on_scalar(half, c) else nc.vector.tensor_copy)
+                at(n, 9, quantize_g, half, c)
+        for n in range(STEPS):
+            at(n - (n % 2 if MX_PAIRED and n >= 4 else 0), 0, multiply, n)
+            at(n, 0.5, middle, n)
+        for pair in range(B_BUFS, PAIRS):
+            group = group_of[pair - B_BUFS]
+            at(4 * (first_pair[group] + GROUP_PAIRS[group]), 0, load_b, pair)
+        n = 0
+        for m, (group, half, i) in enumerate(back_items):
+            size = GROUP_PAIRS[group]
+            n = max(n + 1, 4 * first_pair[group] + 2 * size * (half + 1) + BACK_LAG)
+            at(n, BACK_PHASE, turn_back, m)
+            at(n + Y_LAG, Y_PHASE, threshold, m)
+            if m % 2 == 1:
+                at(n + Y_LAG + 1, 4 if round_y_engine(m // 2) != "gpsimd" else -1, round_y, m // 2)
+                at(n + Y_LAG + 2, 2, turn_y, m // 2)
+                at(n + Y_LAG + (4 if n < STEPS else 3), 3, quantize_y, m // 2)
+        for key in sorted(plan):
+            for fn, args in plan[key]:
+                fn(*args)

@@ -21,46 +21,35 @@ P = 128
 HALF = 512
 HALVES = K // HALF
 CHUNKS = K // P
+QUARTER = 2 * P
+QUARTERS = K // QUARTER
 PAIR = 2 * P
 PAIRS = T // PAIR
-QUARTER = 2 * P
-STEPS = 4 * PAIRS
-GROUP_PAIRS = (1,) * 8
-B_BUFS = 5
-X32_BUFS = 8
-XC_BUFS = 3
-TERM_BUFS = 7
+TILES = T // P
+STAGES = PAIRS * QUARTERS
+PIECES = PAIRS * HALVES
+
+SCALAR_BLOCKS = 5
+X_LEAD = 4
+Y_LAG = 2
+EARLY_TILES = 4
 SCALE_PAIRS = 2
-Y_LAG = 0
-MX_PAIRED = False
+B_BUFS = 4
+STAGING_BUFS = 8
 
-
-def front_step(tile):
-    return 2*tile-8 if tile>3 else tile-3
-
-
-def g_step(half, c):
-    return c-2
-
-
-def g_on_scalar(half, c):
-    return half==1
-
-
-def widen_on_scalar(tile, j):
-    return tile==1
-
-
-def round_x_engine(tile):
-    return "vector"
-
-
-def round_y_engine(mp):
-    return "vector"
-
-
-def fused(n):
-    return False
+(
+    ROUND_LAST,
+    QUANTIZE,
+    INTERLEAVE_VECTOR,
+    WIDEN_VECTOR,
+    ROUND_GPSIMD,
+    MIDDLE,
+    TURN_BACK,
+    TURN_WORDS,
+    INTERLEAVE_SCALAR,
+    WIDEN_SCALAR,
+    THRESHOLD,
+) = range(11)
 
 
 def tile_ista_step_fp8_codes_b5_kernel(tc, X_bytes, X_scale, G, B, step, gain, out_0, out_1, out_2):
@@ -68,368 +57,344 @@ def tile_ista_step_fp8_codes_b5_kernel(tc, X_bytes, X_scale, G, B, step, gain, o
 
     with ExitStack() as ctx:
         keep = ctx.enter_context(tc.tile_pool(name="keep", bufs=1))
-        work = ctx.enter_context(tc.tile_pool(name="work", bufs=2))
-        psum = ctx.enter_context(tc.psum_pool(name="psum", bufs=8))
-        ctx.enter_context(tc.manual_schedule(engines={mybir.EngineType.PE, mybir.EngineType.SP}))
+        work = ctx.enter_context(tc.tile_pool(name="work", bufs=3))
+        psum = ctx.enter_context(tc.psum_pool(name="psum", bufs=6))
+        ctx.enter_context(tc.manual_schedule())
 
-        def bank(dtype):
+        def transpose_bank(dtype):
             return psum.tile([P, HALF], dtype, name="bank", tag="bank")
 
-        ident_f32 = keep.tile([P, P], F32)
-        ident_bf16 = keep.tile([P, P], BF16)
-        coef_rows = keep.tile([P, P], BF16)
-        warm = keep.tile([P, 1], F32)
-        warm_out = keep.tile([P, 1], F32)
-        nc.vector.memset(coef_rows[:], 0.0)
-        nc.vector.memset(warm[:], 0.0)
-        nc.scalar.activation(out=warm_out[:], in_=warm[:], func=ACT.Relu)
-        make_identity(nc, ident_f32[:])
-        make_identity(nc, ident_bf16[:])
+        def pair_rows(matrix, pair):
+            return matrix[pair * PAIR : (pair + 1) * PAIR, :].rearrange("(i p) n -> p i n", p=P)
 
-        first_scale = keep.tile([P, 2 * CHUNKS], F32)
-        x_scale = keep.tile([P, PAIRS - 1, 2 * CHUNKS], F32)
+        scale_rows = X_scale.rearrange("(i p) j -> p i j", p=P)
+        early_scale = keep.tile([P, EARLY_TILES, CHUNKS], F32)
+        late_scale = keep.tile([P, TILES - EARLY_TILES, CHUNKS], F32)
         x_bytes, g_raw, b_rows = {}, {}, {}
 
         def load_x(pair):
-            x_bytes[pair] = keep.tile([P, 2 * K], U8, name="x_bytes", tag="x_bytes", bufs=T // PAIR)
-            rows = X_bytes[pair * PAIR : (pair + 1) * PAIR, :]
-            nc.sync.dma_start(out=x_bytes[pair][:], in_=rows.rearrange("(p i) k -> p (i k)", i=2))
+            x_bytes[pair] = keep.tile([P, 2, K], U8, name="x_bytes", tag="x_bytes", bufs=PAIRS)
+            nc.sync.dma_start(out=x_bytes[pair][:], in_=pair_rows(X_bytes, pair))
 
         def load_g(half, first, last):
-            width = (last - first) * QUARTER
-            raw = keep.tile([P, 4, width], BF16, name="g_raw", tag="g_raw%d_%d" % (half, first))
+            raw = keep.tile([P, 4, (last - first) * QUARTER], BF16, name="g_raw", tag="g_raw_%d_%d" % (half, first))
             block = G[half * HALF : (half + 1) * HALF, first * QUARTER : last * QUARTER]
             nc.sync.dma_start(out=raw[:], in_=block.rearrange("(p t) n -> p t n", t=4))
-            for c in range(first, last):
-                g_raw[half, c] = raw[:, :, (c - first) * QUARTER : (c - first + 1) * QUARTER]
+            for quarter in range(first, last):
+                g_raw[half, quarter] = raw[:, :, (quarter - first) * QUARTER : (quarter - first + 1) * QUARTER]
 
         def load_b(pair):
-            b_rows[pair] = work.tile([P, 2 * K], BF16, name="b_rows", tag="b_rows", bufs=B_BUFS)
-            rows = B[pair * PAIR : (pair + 1) * PAIR, :]
-            nc.sync.dma_start(out=b_rows[pair][:], in_=rows.rearrange("(p i) n -> p (i n)", i=2))
+            b_rows[pair] = work.tile([P, 2, K], BF16, name="b_rows", tag="b_rows", bufs=B_BUFS)
+            nc.sync.dma_start(out=b_rows[pair][:], in_=pair_rows(B, pair))
 
-        scale_rows = X_scale.rearrange("(q p i) j -> p q (i j)", p=P, i=2)
+        nc.scalar.dma_start(out=early_scale[:], in_=scale_rows[:, :EARLY_TILES, :])
+
+        ident_f32 = keep.tile([P, P], F32)
+        ident_bf16 = keep.tile([P, P], BF16)
+        make_identity(nc, ident_f32[:])
+        nc.scalar.activation(out=ident_bf16[:], in_=ident_f32[:], func=ACT.Relu)
+
+        factor_rows = keep.tile([P, P], BF16)
+        nc.vector.memset(factor_rows[:], 0.0)
+        nc.gpsimd.dma_start(out=factor_rows[0:CHUNKS, :], in_=step.rearrange("o (j p) -> (o j) p", p=P))
+        nc.gpsimd.dma_start(out=factor_rows[CHUNKS : 2 * CHUNKS, :], in_=gain.rearrange("o (j p) -> (o j) p", p=P))
+
         load_x(0)
-        nc.sync.dma_start(out=first_scale[:], in_=scale_rows[:, 0, :])
         load_g(0, 0, 1)
         load_g(1, 0, 1)
-        nc.sync.dma_start(out=coef_rows[0:CHUNKS, :], in_=step.rearrange("o (j p) -> (o j) p", p=P))
-        nc.sync.dma_start(out=coef_rows[CHUNKS : 2 * CHUNKS, :], in_=gain.rearrange("o (j p) -> (o j) p", p=P))
-        load_b(0)
         load_g(0, 1, 2)
         load_g(1, 1, 2)
         load_x(1)
-        nc.sync.dma_start(out=x_scale[:], in_=scale_rows[:, 1:, :])
-        load_g(0, 2, 4)
-        load_g(1, 2, 4)
+        load_b(0)
+        load_g(0, 2, QUARTERS)
+        load_g(1, 2, QUARTERS)
         load_x(2)
+        nc.sync.dma_start(out=late_scale[:], in_=scale_rows[:, EARLY_TILES:, :])
         load_b(1)
         load_x(3)
         load_b(2)
         for pair in range(4, PAIRS):
             load_x(pair)
-        for pair in range(3, B_BUFS):
-            load_b(pair)
+        load_b(3)
 
-        coef = keep.tile([P, 2 * CHUNKS], F32)
+        factors = keep.tile([P, 2 * CHUNKS], F32)
         neg_step = keep.tile([P, CHUNKS], F32)
 
-        def make_coefficients():
-            turned = bank(BF16)
-            nc.tensor.transpose(turned[:, 0:P], coef_rows[:], ident_bf16[:])
-            nc.vector.tensor_copy(out=coef[:], in_=turned[:, 0 : 2 * CHUNKS])
+        def make_factors():
+            turned = transpose_bank(BF16)
+            nc.tensor.transpose(turned[:, 0:P], factor_rows[:], ident_bf16[:])
+            nc.vector.tensor_copy(out=factors[:], in_=turned[:, 0 : 2 * CHUNKS])
             nc.vector.tensor_scalar(
                 out=neg_step[:], in0=turned[:, 0:CHUNKS], scalar1=-1.0, scalar2=None, op0=ALU.mult
             )
 
         g_grouped, g_codes, g_scales = {}, {}, {}
 
-        def interleave_g(half, c, copy):
-            g_grouped[half, c] = work.tile([P, QUARTER, 4], BF16, name="g_grouped", tag="g_grouped", bufs=4, align_bytes=64)
+        def interleave_g(half, quarter):
+            copy = nc.vector.tensor_copy if half == 0 else nc.scalar.copy
+            g_grouped[half, quarter] = work.tile(
+                [P, QUARTER, 4], BF16, name="g_grouped", tag="g_grouped", bufs=4, align_bytes=64
+            )
             copy(
-                out=g_grouped[half, c][:].rearrange("p (c i) t -> p c t i", i=4),
-                in_=g_raw[half, c].rearrange("p t (c i) -> p c t i", i=4),
+                out=g_grouped[half, quarter][:].rearrange("p (c i) t -> p c t i", i=4),
+                in_=g_raw[half, quarter].rearrange("p t (c i) -> p c t i", i=4),
             )
 
-        def quantize_g(half, c):
-            g_codes[half, c] = keep.tile([P, QUARTER], U32, name="g_codes", tag="g_codes", bufs=8, align_bytes=64)
-            g_scales[half, c] = keep.tile([P, QUARTER], U8, name="g_scales", tag="g_scales", bufs=8, align_bytes=64)
+        def quantize_g(half, quarter):
+            count = HALVES * QUARTERS
+            g_codes[half, quarter] = keep.tile(
+                [P, QUARTER], U32, name="g_codes", tag="g_codes", bufs=count, align_bytes=64
+            )
+            g_scales[half, quarter] = keep.tile(
+                [P, QUARTER], U8, name="g_scales", tag="g_scales", bufs=count, align_bytes=64
+            )
             nc.vector.quantize_mx(
-                out=g_codes[half, c][:].bitcast(FP8X4),
-                scales=g_scales[half, c][:],
-                in_=g_grouped[half, c][:].rearrange("p n t -> p (n t)"),
+                out=g_codes[half, quarter][:].bitcast(FP8X4),
+                scales=g_scales[half, quarter][:],
+                in_=g_grouped[half, quarter][:].rearrange("p n t -> p (n t)"),
             )
 
-        group_of, first_pair = [], []
-        for group, size in enumerate(GROUP_PAIRS):
-            first_pair.append(len(group_of))
-            group_of.extend([group] * size)
+        staging, x_words, y_words = {}, {}, {}
 
-        x32, x_sorted, x_grouped, x_codes, x_scales = {}, {}, {}, {}, {}
+        def staged(window):
+            if window not in staging:
+                staging[window] = work.tile([P, 2 * K], F32, name="staging", tag="staging", bufs=STAGING_BUFS)
+            return staging[window]
 
-        def widen_x(tile):
-            pair, i = divmod(tile, 2)
-            scales = first_scale[:] if pair == 0 else x_scale[:, pair - 1, :]
-            x32[tile] = work.tile([P, K], F32, name="x32", tag="x32", bufs=X32_BUFS)
-            for j in range(CHUNKS):
-                values = x32[tile][:, j * P : (j + 1) * P]
-                codes = x_bytes[pair][:, i * K + j * P : i * K + (j + 1) * P].bitcast(FP8)
-                scale = scales[:, i * CHUNKS + j : i * CHUNKS + j + 1]
-                if widen_on_scalar(tile, j):
-                    nc.scalar.activation(out=values, in_=codes, func=ACT.Copy, scale=scale)
+        def x_values(tile):
+            return staged(tile - X_LEAD)[:, :K]
+
+        def y_values(piece):
+            return staged(piece + Y_LAG)[:, K:].rearrange("p (i n) -> p i n", i=2)
+
+        def widen_x(tile, blocks, on_scalar):
+            scales = early_scale[:, tile, :] if tile < EARLY_TILES else late_scale[:, tile - EARLY_TILES, :]
+            for j in blocks:
+                values = x_values(tile)[:, j * P : (j + 1) * P]
+                fp8_values = x_bytes[tile // 2][:, tile % 2, j * P : (j + 1) * P].bitcast(FP8)
+                if on_scalar:
+                    nc.scalar.activation(out=values, in_=fp8_values, func=ACT.Copy, scale=scales[:, j : j + 1])
                 else:
-                    nc.vector.tensor_scalar(out=values, in0=codes, scalar1=scale, scalar2=None, op0=ALU.mult)
+                    nc.vector.tensor_scalar(
+                        out=values, in0=fp8_values, scalar1=scales[:, j : j + 1], scalar2=None, op0=ALU.mult
+                    )
 
-        def round_sorted(rounded, values, engine):
-            rounded = rounded.rearrange("p (u w e) -> p u w e", u=2, e=2)
-            values = values.rearrange("p (w u e) -> p u w e", u=2, e=2)
-            if engine == "gpsimd":
-                nc.gpsimd.tensor_scalar(out=rounded, in0=values, scalar1=1.0, scalar2=1.0, op0=ALU.mult, op1=ALU.mult)
-            elif engine == "scalar":
-                nc.scalar.copy(out=rounded, in_=values)
+        def round_window(window, on_gpsimd):
+            tile, piece = window + X_LEAD, window - Y_LAG
+            has_x, has_y = tile < TILES, piece >= 0
+            values = staged(window)[:, (0 if has_x else K) : (2 * K if has_y else K)]
+            rounded = work.tile([P, values.shape[1]], BF16, name="rounded", tag="rounded")
+            in_order = values.rearrange("p (w u e) -> p u w e", u=2, e=2)
+            sorted_out = rounded[:].rearrange("p (u w e) -> p u w e", u=2, e=2)
+            if on_gpsimd:
+                nc.gpsimd.tensor_scalar(out=sorted_out, in0=in_order, scalar1=1.0, scalar2=1.0, op0=ALU.mult, op1=ALU.mult)
             else:
-                nc.vector.tensor_copy(out=rounded, in_=values)
+                nc.vector.tensor_copy(out=sorted_out, in_=in_order)
+            runs = rounded[:].bitcast(F32).rearrange("p (u a w) -> p a u w", u=2, w=P)
+            if has_x:
+                x_words[tile] = runs[:, 0:2, :, :]
+            if has_y:
+                y_words[piece] = runs[:, 2:4, :, :] if has_x else runs
 
-        def turn_words(rounded):
-            words = rounded.bitcast(F32)
-            turned = bank(F32)
+        def turn_words(name, runs):
+            turned = transpose_bank(F32)
             for a in range(2):
                 for u in range(2):
-                    nc.tensor.transpose(
-                        turned[:, (2 * a + u) * P : (2 * a + u + 1) * P],
-                        words[:, (2 * u + a) * P : (2 * u + a + 1) * P],
-                        ident_f32[:],
-                    )
-            return turned
+                    slot = 2 * a + u
+                    nc.tensor.transpose(turned[:, slot * P : (slot + 1) * P], runs[:, a, u, :], ident_f32[:])
+            grouped = work.tile([P, K], BF16, name=name, tag=name, align_bytes=64)
+            nc.scalar.copy(
+                out=grouped[:].bitcast(F32).rearrange("p (a c u) -> p a c u", a=2, u=2),
+                in_=turned[:].rearrange("p (a u c) -> p a c u", a=2, u=2),
+            )
+            return grouped
 
-        def round_x(tile):
-            x_sorted[tile] = work.tile([P, K], BF16, name="x_sorted", tag="x_sorted")
-            round_sorted(x_sorted[tile][:], x32[tile][:], round_x_engine(tile))
+        x_grouped, x_codes, x_scales = {}, {}, {}
 
         def turn_x(tile):
-            turned = turn_words(x_sorted[tile][:])
-            x_grouped[tile] = work.tile([P, K], BF16, name="x_grouped", tag="x_grouped", align_bytes=64)
-            nc.scalar.copy(
-                out=x_grouped[tile][:].bitcast(F32).rearrange("p (h c u) -> p h c u", h=2, u=2),
-                in_=turned[:].rearrange("p (h u c) -> p h c u", h=2, u=2),
-            )
+            x_grouped[tile] = turn_words("x_grouped", x_words[tile])
 
         def quantize_x(tile):
-            group = group_of[tile // 2]
-            i = tile - 2 * first_pair[group]
-            width = GROUP_PAIRS[group] * PAIR
+            pair, i = divmod(tile, 2)
             if i == 0:
-                x_codes[group] = work.tile([P, HALVES, width], U32, name="x_codes", tag="x_codes", bufs=XC_BUFS, align_bytes=64)
-                x_scales[group] = work.tile([P, HALVES, width], U8, name="x_scales", tag="x_scales", bufs=XC_BUFS, align_bytes=64)
+                x_codes[pair] = work.tile([P, HALVES, PAIR], U32, name="x_codes", tag="x_codes", align_bytes=64)
+                x_scales[pair] = work.tile([P, HALVES, PAIR], U8, name="x_scales", tag="x_scales", align_bytes=64)
             for half in range(HALVES):
                 nc.vector.quantize_mx(
-                    out=x_codes[group][:, half, i * P : (i + 1) * P].bitcast(FP8X4),
-                    scales=x_scales[group][:, half, i * P : (i + 1) * P],
+                    out=x_codes[pair][:, half, i * P : (i + 1) * P].bitcast(FP8X4),
+                    scales=x_scales[pair][:, half, i * P : (i + 1) * P],
                     in_=x_grouped[tile][:, half * HALF : (half + 1) * HALF],
                 )
 
-        terms, products = {}, {}
+        u_turned = {}
 
-        def chunks_of(n):
-            group = group_of[n // 4]
-            size = GROUP_PAIRS[group]
-            count = 2 // size
-            first = (n - 4 * first_pair[group]) * count
-            return group, size * PAIR, range(first, first + count)
-
-        def multiply(n):
-            group, width, chunks = chunks_of(n)
-            products[n] = bank(F32)
-            for slot, j in enumerate(chunks):
-                c, jj = divmod(j, 2)
+        def middle(stage):
+            pair, quarter = divmod(stage, QUARTERS)
+            spans = [(jj, 2 * quarter + jj, slice(jj * PAIR, (jj + 1) * PAIR)) for jj in range(2)]
+            product = psum.tile([P, HALF], F32, name="product", tag="product", bufs=2)
+            b_turned = transpose_bank(BF16)
+            x_turned = transpose_bank(F32)
+            for jj, j, cols in spans:
                 for half in range(HALVES):
                     nc.tensor.matmul_mx(
-                        out=products[n][:, slot * width : (slot + 1) * width],
-                        lhsT=g_codes[half, c][:, jj * P : (jj + 1) * P].bitcast(FP8X4),
-                        lhsT_scale=g_scales[half, c][:, jj * P : (jj + 1) * P],
-                        rhs=x_codes[group][:, half, :].bitcast(FP8X4),
-                        rhs_scale=x_scales[group][:, half, :],
+                        out=product[:, cols],
+                        lhsT=g_codes[half, quarter][:, jj * P : (jj + 1) * P].bitcast(FP8X4),
+                        lhsT_scale=g_scales[half, quarter][:, jj * P : (jj + 1) * P],
+                        rhs=x_codes[pair][:, half, :].bitcast(FP8X4),
+                        rhs_scale=x_scales[pair][:, half, :],
                         start=(half == 0),
                         stop=(half == HALVES - 1),
                     )
-
-        def middle(n):
-            group, width, chunks = chunks_of(n)
-            group_tiles = range(2 * first_pair[group], 2 * first_pair[group] + width // P)
-            b_turned = bank(BF16)
-            x_turned = bank(F32)
-            for slot, j in enumerate(chunks):
-                for i, tile in enumerate(group_tiles):
-                    start = (tile % 2) * K + j * P
-                    cols = slice(slot * width + i * P, slot * width + (i + 1) * P)
-                    nc.tensor.transpose(b_turned[:, cols], b_rows[tile // 2][:, start : start + P], ident_bf16[:])
-            for slot, j in enumerate(chunks):
-                for i, tile in enumerate(group_tiles):
-                    cols = slice(slot * width + i * P, slot * width + (i + 1) * P)
-                    nc.tensor.transpose(x_turned[:, cols], x32[tile][:, j * P : (j + 1) * P], ident_f32[:])
-            p_term = work.tile([P, HALF], F32, name="p_term", tag="p_term", bufs=3)
-            px_term = work.tile([P, HALF], F32, name="px_term", tag="px_term", bufs=TERM_BUFS)
-            b_term = work.tile([P, HALF], F32, name="b_term", tag="b_term", bufs=TERM_BUFS)
-            spans = [(slice(slot * width, (slot + 1) * width), j) for slot, j in enumerate(chunks)]
-            for cols, j in spans:
-                nc.scalar.activation(
-                    out=p_term[:, cols], in_=products[n][:, cols], func=ACT.Copy, scale=neg_step[:, j : j + 1]
-                )
-            if not fused(n):
-                for cols, j in spans:
-                    nc.scalar.activation(
-                        out=b_term[:, cols], in_=b_turned[:, cols], func=ACT.Copy, scale=coef[:, j : j + 1]
+            for jj, j, cols in spans:
+                for i in range(2):
+                    nc.tensor.transpose(
+                        b_turned[:, cols][:, i * P : (i + 1) * P], b_rows[pair][:, i, j * P : (j + 1) * P], ident_bf16[:]
                     )
-            for cols, j in spans:
+            for jj, j, cols in spans:
+                for i in range(2):
+                    nc.tensor.transpose(
+                        x_turned[:, cols][:, i * P : (i + 1) * P],
+                        x_values(2 * pair + i)[:, j * P : (j + 1) * P],
+                        ident_f32[:],
+                    )
+            p_term = work.tile([P, HALF], F32, name="p_term", tag="p_term")
+            px_term = work.tile([P, HALF], F32, name="px_term", tag="px_term")
+            u_term = work.tile([P, HALF], F32, name="u_term", tag="u_term", bufs=6)
+            for jj, j, cols in spans:
+                nc.scalar.activation(
+                    out=p_term[:, cols], in_=product[:, cols], func=ACT.Copy, scale=neg_step[:, j : j + 1]
+                )
+            for jj, j, cols in spans:
                 nc.vector.scalar_tensor_tensor(
                     out=px_term[:, cols],
                     in0=x_turned[:, cols],
-                    scalar=coef[:, CHUNKS + j : CHUNKS + j + 1],
+                    scalar=factors[:, CHUNKS + j : CHUNKS + j + 1],
                     in1=p_term[:, cols],
                     op0=ALU.mult,
                     op1=ALU.add,
                 )
-            for cols, j in spans:
-                if fused(n):
-                    nc.vector.scalar_tensor_tensor(
-                        out=b_term[:, cols],
-                        in0=b_turned[:, cols],
-                        scalar=coef[:, j : j + 1],
-                        in1=px_term[:, cols],
-                        op0=ALU.mult,
-                        op1=ALU.add,
-                    )
-                    terms[group, j] = [b_term[:, cols]]
-                else:
-                    terms[group, j] = [px_term[:, cols], b_term[:, cols]]
+            for jj, j, cols in spans:
+                nc.vector.scalar_tensor_tensor(
+                    out=u_term[:, cols],
+                    in0=b_turned[:, cols],
+                    scalar=factors[:, j : j + 1],
+                    in1=px_term[:, cols],
+                    op0=ALU.mult,
+                    op1=ALU.add,
+                )
+                u_turned[pair, j] = u_term[:, cols]
 
-        u_bank, above, y_rows, y_sorted, y_grouped, y_scales = {}, {}, {}, {}, {}, {}
+        u_rows, above, y_grouped, y_scales = {}, {}, {}, {}
 
-        back_items = []
-        for group, size in enumerate(GROUP_PAIRS):
-            for half in range(HALVES):
-                for i in range(2 * size):
-                    back_items.append((group, half, i))
+        def turn_back(piece, i):
+            pair, half = divmod(piece, HALVES)
+            u_rows[piece, i] = transpose_bank(F32)
+            for jj in range(HALF // P):
+                nc.tensor.transpose(
+                    u_rows[piece, i][:, jj * P : (jj + 1) * P],
+                    u_turned[pair, half * (HALF // P) + jj][:, i * P : (i + 1) * P],
+                    ident_f32[:],
+                )
+            above[piece, i] = work.tile([P, HALF], F32, name="above", tag="above")
+            nc.scalar.activation(out=above[piece, i][:], in_=u_rows[piece, i][:], func=ACT.Relu, bias=-THETA)
 
-        def turn_back(m):
-            group, half, i = back_items[m]
-            u_bank[m] = bank(F32)
-            for jj in range(4):
-                addends = terms[group, half * 4 + jj]
-                for a, term in enumerate(addends):
-                    nc.tensor.matmul(
-                        out=u_bank[m][:, jj * P : (jj + 1) * P],
-                        lhsT=term[:, i * P : (i + 1) * P],
-                        rhs=ident_f32[:],
-                        is_transpose=True,
-                        start=(a == 0),
-                        stop=(a == len(addends) - 1),
-                    )
-            above[m] = work.tile([P, HALF], F32, name="above", tag="above", bufs=3)
-            nc.scalar.activation(out=above[m][:], in_=u_bank[m][:], func=ACT.Relu, bias=-THETA)
-
-        def threshold(m):
-            group, half, i = back_items[m]
-            if i % 2 == 0:
-                y_rows[m // 2] = work.tile([P, 2, HALF], F32, name="y_rows", tag="y_rows", bufs=3)
+        def threshold(piece, i):
+            pair, half = divmod(piece, HALVES)
             nc.vector.scalar_tensor_tensor(
-                out=y_rows[m // 2][:, i % 2, :],
-                in0=u_bank[m][:],
+                out=y_values(piece)[:, i, :],
+                in0=u_rows[piece, i][:],
                 scalar=THETA,
-                in1=above[m][:],
+                in1=above[piece, i][:],
                 op0=ALU.add,
                 op1=ALU.min,
             )
-            if i % 2 == 1:
-                first = (first_pair[group] + i // 2) * PAIR
-                rows = out_0[first : first + PAIR, half * HALF : (half + 1) * HALF]
-                nc.sync.dma_start(out=rows.rearrange("(p i) n -> p i n", i=2), in_=y_rows[m // 2][:])
+            if i == 1:
+                nc.sync.dma_start(out=pair_rows(out_0, pair)[:, :, half * HALF : (half + 1) * HALF], in_=y_values(piece))
 
-        def round_y(mp):
-            y_sorted[mp] = work.tile([P, K], BF16, name="y_sorted", tag="y_sorted")
-            round_sorted(y_sorted[mp][:], y_rows[mp][:].rearrange("p i n -> p (i n)"), round_y_engine(mp))
+        def turn_y(piece):
+            y_grouped[piece] = turn_words("y_grouped", y_words[piece])
 
-        def turn_y(mp):
-            turned = turn_words(y_sorted[mp][:])
-            y_grouped[mp] = work.tile([P, K], BF16, name="y_grouped", tag="y_grouped", align_bytes=64)
-            nc.scalar.copy(
-                out=y_grouped[mp][:].bitcast(F32).rearrange("p (c a) -> p c a", a=4),
-                in_=turned[:].rearrange("p (a c) -> p c a", a=4),
-            )
-
-        def quantize_y(mp):
-            group, half, i = back_items[2 * mp]
-            pair = first_pair[group] + i // 2
-            store, q = divmod(pair, SCALE_PAIRS)
-            if store not in y_scales:
-                y_scales[store] = work.tile([P, HALVES, SCALE_PAIRS * PAIR], U8, name="y_scales", tag="y_scales", align_bytes=64)
-            y_codes = work.tile([P, PAIR], U32, name="y_codes", tag="y_codes", bufs=3, align_bytes=64)
+        def quantize_y(piece):
+            pair, half = divmod(piece, HALVES)
+            batch, place = divmod(pair, SCALE_PAIRS)
+            if half == 0 and place == 0:
+                y_scales[batch] = work.tile(
+                    [P, HALVES, SCALE_PAIRS * PAIR], U8, name="y_scales", tag="y_scales", bufs=2, align_bytes=64
+                )
+            y_codes = work.tile([P, PAIR], U32, name="y_codes", tag="y_codes", align_bytes=64)
             nc.vector.quantize_mx(
                 out=y_codes[:].bitcast(FP8X4),
-                scales=y_scales[store][:, half, q * PAIR : (q + 1) * PAIR],
-                in_=y_grouped[mp][:],
+                scales=y_scales[batch][:, half, place * PAIR : (place + 1) * PAIR],
+                in_=y_grouped[piece][:],
             )
-            first = pair * PAIR
-            words = out_1[half, :, first : first + PAIR, :].rearrange("p m t -> p (m t)")
-            nc.sync.dma_start(out=words.bitcast(I32), in_=y_codes[:].bitcast(I32))
-            if half == HALVES - 1 and q == SCALE_PAIRS - 1:
-                planes = out_2[:, :, store * SCALE_PAIRS * PAIR : (store + 1) * SCALE_PAIRS * PAIR].bitcast(I32)
+            code_rows = out_1[half, :, pair * PAIR : (pair + 1) * PAIR, :].rearrange("p m t -> p (m t)")
+            nc.sync.dma_start(out=code_rows.bitcast(I32), in_=y_codes[:].bitcast(I32))
+            if half == HALVES - 1 and place == SCALE_PAIRS - 1:
+                tokens = slice(batch * SCALE_PAIRS * PAIR, (batch + 1) * SCALE_PAIRS * PAIR)
+                scale_planes = out_2[:, :, tokens].bitcast(I32)
                 for quadrant in range(4):
                     nc.sync.dma_start(
-                        out=planes[:, 4 * quadrant : 4 * quadrant + 4, :].rearrange("h r m -> r h m"),
-                        in_=y_scales[store][32 * quadrant : 32 * quadrant + 4, :, :].bitcast(I32),
+                        out=scale_planes[:, 4 * quadrant : 4 * quadrant + 4, :].rearrange("h r m -> r h m"),
+                        in_=y_scales[batch][32 * quadrant : 32 * quadrant + 4, :, :].bitcast(I32),
                     )
 
-        RX_PHASE, BACK_LAG, BACK_PHASE, Y_PHASE = 4, 0, 1, 6
-        plan = {}
-
-        def at(n, phase, fn, *args):
-            plan.setdefault((n, phase), []).append((fn, args))
-
-        widen_x(0)
-        widen_x(1)
-        interleave_g(0, 0, nc.vector.tensor_copy)
-        interleave_g(1, 0, nc.scalar.copy)
-        round_x(0)
-        round_x(1)
+        all_blocks = range(CHUNKS)
+        widen_x(0, all_blocks, False)
+        widen_x(1, all_blocks, True)
+        interleave_g(0, 0)
+        interleave_g(1, 0)
+        round_window(0 - X_LEAD, False)
+        round_window(1 - X_LEAD, False)
         turn_x(0)
         turn_x(1)
-        make_coefficients()
         quantize_g(0, 0)
+        interleave_g(0, 1)
+        interleave_g(1, 1)
         quantize_g(1, 0)
-        interleave_g(0, 1, nc.vector.tensor_copy)
-        interleave_g(1, 1, nc.scalar.copy)
+        make_factors()
         quantize_x(0)
         quantize_x(1)
         quantize_g(0, 1)
-        for tile in range(2, 2 * PAIRS):
-            n = front_step(tile)
-            at(n, 5, widen_x, tile)
-            at(n + 1, RX_PHASE if round_x_engine(tile) != "gpsimd" else -1, round_x, tile)
-            at(n + 2, 2, turn_x, tile)
-            at(n + 3, 3, quantize_x, tile)
-        at(-1, 9, quantize_g, 1, 1)
-        for c in range(2, 4):
+        widen_x(2, all_blocks, False)
+        round_window(2 - X_LEAD, False)
+
+        plan = {}
+
+        def at(stage, phase, call, *args):
+            plan.setdefault((stage, phase), []).append((call, args))
+
+        at(0, TURN_WORDS, turn_x, 2)
+        at(1, QUANTIZE, quantize_x, 2)
+        at(0, QUANTIZE, quantize_g, 1, 1)
+        for quarter in range(2, QUARTERS):
+            at(quarter - 2, INTERLEAVE_VECTOR, interleave_g, 0, quarter)
+            at(quarter - 2, INTERLEAVE_SCALAR, interleave_g, 1, quarter)
             for half in range(HALVES):
-                n = g_step(half, c)
-                at(n, 4, interleave_g, half, c, nc.scalar.copy if g_on_scalar(half, c) else nc.vector.tensor_copy)
-                at(n, 9, quantize_g, half, c)
-        for n in range(STEPS):
-            at(n - (n % 2 if MX_PAIRED and n >= 4 else 0), 0, multiply, n)
-            at(n, 0.5, middle, n)
+                at(quarter - 1, QUANTIZE, quantize_g, half, quarter)
+        for tile in range(3, TILES):
+            window = tile - X_LEAD
+            stage = max(2 * window, window + 1)
+            at(stage - 1, WIDEN_SCALAR, widen_x, tile, range(SCALAR_BLOCKS), True)
+            at(stage, WIDEN_VECTOR, widen_x, tile, range(SCALAR_BLOCKS, CHUNKS), False)
+            at(stage, ROUND_GPSIMD, round_window, window, True)
+            at(max(2 * window + 2, stage + 1), TURN_WORDS, turn_x, tile)
+            at(2 * window + 4, QUANTIZE, quantize_x, tile)
+        last_window = PIECES - 1 + Y_LAG
+        for window in range(TILES - X_LEAD, last_window):
+            at(2 * window, ROUND_GPSIMD, round_window, window, True)
+        at(2 * last_window, ROUND_LAST, round_window, last_window, False)
+        for stage in range(STAGES):
+            at(stage, MIDDLE, middle, stage)
         for pair in range(B_BUFS, PAIRS):
-            group = group_of[pair - B_BUFS]
-            at(4 * (first_pair[group] + GROUP_PAIRS[group]), 0, load_b, pair)
-        n = 0
-        for m, (group, half, i) in enumerate(back_items):
-            size = GROUP_PAIRS[group]
-            n = max(n + 1, 4 * first_pair[group] + 2 * size * (half + 1) + BACK_LAG)
-            at(n, BACK_PHASE, turn_back, m)
-            at(n + Y_LAG, Y_PHASE, threshold, m)
-            if m % 2 == 1:
-                at(n + Y_LAG + 1, 4 if round_y_engine(m // 2) != "gpsimd" else -1, round_y, m // 2)
-                at(n + Y_LAG + 2, 2, turn_y, m // 2)
-                at(n + Y_LAG + (4 if n < STEPS else 3), 3, quantize_y, m // 2)
+            at(QUARTERS * (pair - B_BUFS + 1), MIDDLE, load_b, pair)
+        for piece in range(PIECES):
+            for i in range(2):
+                at(2 * (piece + 1) + i, TURN_BACK, turn_back, piece, i)
+                at(2 * (piece + 1) + i, THRESHOLD, threshold, piece, i)
+            stage = 2 * (piece + Y_LAG)
+            wait = 3 if stage < STAGES else 1
+            at(stage + wait, TURN_WORDS, turn_y, piece)
+            at(stage + wait + 1, QUANTIZE, quantize_y, piece)
         for key in sorted(plan):
-            for fn, args in plan[key]:
-                fn(*args)
+            for call, args in plan[key]:
+                call(*args)

@@ -47,9 +47,11 @@ STAGING_BUFS = 8
     TURN_BACK,
     TURN_WORDS,
     INTERLEAVE_SCALAR,
+    ROUND_VECTOR,
     WIDEN_SCALAR,
+    QUANTIZE_LATE,
     THRESHOLD,
-) = range(11)
+) = range(13)
 
 
 def tile_ista_step_fp8_codes_b5_kernel(tc, X_bytes, X_scale, G, B, step, gain, out_0, out_1, out_2):
@@ -332,8 +334,9 @@ def tile_ista_step_fp8_codes_b5_kernel(tc, X_bytes, X_scale, G, B, step, gain, o
             if half == HALVES - 1 and place == SCALE_PAIRS - 1:
                 tokens = slice(batch * SCALE_PAIRS * PAIR, (batch + 1) * SCALE_PAIRS * PAIR)
                 scale_planes = out_2[:, :, tokens].bitcast(I32)
+                queue = nc.scalar if piece == PIECES - 1 else nc.sync
                 for quadrant in range(4):
-                    nc.sync.dma_start(
+                    queue.dma_start(
                         out=scale_planes[:, 4 * quadrant : 4 * quadrant + 4, :].rearrange("h r m -> r h m"),
                         in_=y_scales[batch][32 * quadrant : 32 * quadrant + 4, :, :].bitcast(I32),
                     )
@@ -371,14 +374,21 @@ def tile_ista_step_fp8_codes_b5_kernel(tc, X_bytes, X_scale, G, B, step, gain, o
             at(quarter - 2, INTERLEAVE_SCALAR, interleave_g, 1, quarter)
             for half in range(HALVES):
                 at(quarter - 1, QUANTIZE, quantize_g, half, quarter)
+        late_stage = 2 * (TILES - X_LEAD)
         for tile in range(3, TILES):
             window = tile - X_LEAD
             stage = max(2 * window, window + 1)
             at(stage - 1, WIDEN_SCALAR, widen_x, tile, range(SCALAR_BLOCKS), True)
             at(stage, WIDEN_VECTOR, widen_x, tile, range(SCALAR_BLOCKS, CHUNKS), False)
-            at(stage, ROUND_GPSIMD, round_window, window, True)
+            if window > 0:
+                at(stage, ROUND_GPSIMD, round_window, window, True)
+            else:
+                at(stage, ROUND_VECTOR, round_window, window, False)
             at(max(2 * window + 2, stage + 1), TURN_WORDS, turn_x, tile)
-            at(2 * window + 4, QUANTIZE, quantize_x, tile)
+            if 2 * window + 4 < late_stage:
+                at(2 * window + 4, QUANTIZE, quantize_x, tile)
+            else:
+                at(2 * window + 3, QUANTIZE_LATE, quantize_x, tile)
         last_window = PIECES - 1 + Y_LAG
         for window in range(TILES - X_LEAD, last_window):
             at(2 * window, ROUND_GPSIMD, round_window, window, True)
@@ -394,7 +404,10 @@ def tile_ista_step_fp8_codes_b5_kernel(tc, X_bytes, X_scale, G, B, step, gain, o
             stage = 2 * (piece + Y_LAG)
             wait = 3 if stage < STAGES else 1
             at(stage + wait, TURN_WORDS, turn_y, piece)
-            at(stage + wait + 1, QUANTIZE, quantize_y, piece)
+            if late_stage <= stage + wait + 1 < STAGES:
+                at(stage + wait + 2, QUANTIZE_LATE, quantize_y, piece)
+            else:
+                at(stage + wait + 1, QUANTIZE, quantize_y, piece)
         for key in sorted(plan):
             for call, args in plan[key]:
                 call(*args)

from contextlib import ExitStack

import concourse.mybir as mybir
from concourse.masks import make_identity

T, K = 2048, 1024
THETA = 0.08
FLOPS = 2 * T * K * K

F32 = mybir.dt.float32
BF16 = mybir.dt.bfloat16
I32 = mybir.dt.int32
U32 = mybir.dt.uint32
U8 = mybir.dt.uint8
FP8 = mybir.dt.float8_e4m3fn
FP8X4 = mybir.dt.float8_e4m3fn_x4
ALU = mybir.AluOpType
ACT = mybir.ActivationFunctionType

P = 128
HALF = 512
HALVES = K // HALF
CHUNKS = K // P
QUARTER = 2 * P
QUARTERS = K // QUARTER
PAIR = 2 * P
PAIRS = T // PAIR
TILES = T // P
STAGES = PAIRS * QUARTERS
PIECES = PAIRS * HALVES

SCALAR_BLOCKS = 5
X_LEAD = 4
Y_LAG = 2
EARLY_TILES = 4
SCALE_PAIRS = 2
B_BUFS = 4
STAGING_BUFS = 8

(
    ROUND_LAST,
    QUANTIZE,
    INTERLEAVE_VECTOR,
    WIDEN_VECTOR,
    ROUND_GPSIMD,
    MIDDLE,
    TURN_BACK,
    TURN_WORDS,
    INTERLEAVE_SCALAR,
    ROUND_VECTOR,
    WIDEN_SCALAR,
    QUANTIZE_LATE,
    THRESHOLD,
) = range(13)


def tile_ista_step_fp8_codes_b5_kernel(tc, X_bytes, X_scale, G, B, step, gain, out_0, out_1, out_2):
    nc = tc.nc

    with ExitStack() as ctx:
        keep = ctx.enter_context(tc.tile_pool(name="keep", bufs=1))
        work = ctx.enter_context(tc.tile_pool(name="work", bufs=3))
        psum = ctx.enter_context(tc.psum_pool(name="psum", bufs=6))
        ctx.enter_context(tc.manual_schedule())

        def transpose_bank(dtype):
            return psum.tile([P, HALF], dtype, name="bank", tag="bank")

        def pair_rows(matrix, pair):
            return matrix[pair * PAIR : (pair + 1) * PAIR, :].rearrange("(i p) n -> p i n", p=P)

        scale_rows = X_scale.rearrange("(i p) j -> p i j", p=P)
        early_scale = keep.tile([P, EARLY_TILES, CHUNKS], F32)
        late_scale = keep.tile([P, TILES - EARLY_TILES, CHUNKS], F32)
        x_bytes, g_raw, b_rows = {}, {}, {}

        def load_x(pair):
            x_bytes[pair] = keep.tile([P, 2, K], U8, name="x_bytes", tag="x_bytes", bufs=PAIRS)
            nc.sync.dma_start(out=x_bytes[pair][:], in_=pair_rows(X_bytes, pair))

        def load_g(half, first, last):
            raw = keep.tile([P, 4, (last - first) * QUARTER], BF16, name="g_raw", tag="g_raw_%d_%d" % (half, first))
            block = G[half * HALF : (half + 1) * HALF, first * QUARTER : last * QUARTER]
            nc.sync.dma_start(out=raw[:], in_=block.rearrange("(p t) n -> p t n", t=4))
            for quarter in range(first, last):
                g_raw[half, quarter] = raw[:, :, (quarter - first) * QUARTER : (quarter - first + 1) * QUARTER]

        def load_b(pair):
            b_rows[pair] = work.tile([P, 2, K], BF16, name="b_rows", tag="b_rows", bufs=B_BUFS)
            nc.sync.dma_start(out=b_rows[pair][:], in_=pair_rows(B, pair))

        nc.scalar.dma_start(out=early_scale[:], in_=scale_rows[:, :EARLY_TILES, :])

        ident_f32 = keep.tile([P, P], F32)
        ident_bf16 = keep.tile([P, P], BF16)
        make_identity(nc, ident_f32[:])
        nc.scalar.activation(out=ident_bf16[:], in_=ident_f32[:], func=ACT.Relu)

        factor_rows = keep.tile([P, P], BF16)
        nc.vector.memset(factor_rows[:], 0.0)
        nc.gpsimd.dma_start(out=factor_rows[0:CHUNKS, :], in_=step.rearrange("o (j p) -> (o j) p", p=P))
        nc.gpsimd.dma_start(out=factor_rows[CHUNKS : 2 * CHUNKS, :], in_=gain.rearrange("o (j p) -> (o j) p", p=P))

        load_x(0)
        load_g(0, 0, 1)
        load_g(1, 0, 1)
        load_g(0, 1, 2)
        load_g(1, 1, 2)
        load_x(1)
        load_b(0)
        load_g(0, 2, QUARTERS)
        load_g(1, 2, QUARTERS)
        load_x(2)
        nc.sync.dma_start(out=late_scale[:], in_=scale_rows[:, EARLY_TILES:, :])
        load_b(1)
        load_x(3)
        load_b(2)
        for pair in range(4, PAIRS):
            load_x(pair)
        load_b(3)

        factors = keep.tile([P, 2 * CHUNKS], F32)
        neg_step = keep.tile([P, CHUNKS], F32)

        def make_factors():
            turned = transpose_bank(BF16)
            nc.tensor.transpose(turned[:, 0:P], factor_rows[:], ident_bf16[:])
            nc.vector.tensor_copy(out=factors[:], in_=turned[:, 0 : 2 * CHUNKS])
            nc.vector.tensor_scalar(
                out=neg_step[:], in0=turned[:, 0:CHUNKS], scalar1=-1.0, scalar2=None, op0=ALU.mult
            )

        g_grouped, g_codes, g_scales = {}, {}, {}

        def interleave_g(half, quarter):
            copy = nc.vector.tensor_copy if half == 0 else nc.scalar.copy
            g_grouped[half, quarter] = work.tile(
                [P, QUARTER, 4], BF16, name="g_grouped", tag="g_grouped", bufs=4, align_bytes=64
            )
            copy(
                out=g_grouped[half, quarter][:].rearrange("p (c i) t -> p c t i", i=4),
                in_=g_raw[half, quarter].rearrange("p t (c i) -> p c t i", i=4),
            )

        def quantize_g(half, quarter):
            count = HALVES * QUARTERS
            g_codes[half, quarter] = keep.tile(
                [P, QUARTER], U32, name="g_codes", tag="g_codes", bufs=count, align_bytes=64
            )
            g_scales[half, quarter] = keep.tile(
                [P, QUARTER], U8, name="g_scales", tag="g_scales", bufs=count, align_bytes=64
            )
            nc.vector.quantize_mx(
                out=g_codes[half, quarter][:].bitcast(FP8X4),
                scales=g_scales[half, quarter][:],
                in_=g_grouped[half, quarter][:].rearrange("p n t -> p (n t)"),
            )

        staging, x_words, y_words = {}, {}, {}

        def staged(window):
            if window not in staging:
                staging[window] = work.tile([P, 2 * K], F32, name="staging", tag="staging", bufs=STAGING_BUFS)
            return staging[window]

        def x_values(tile):
            return staged(tile - X_LEAD)[:, :K]

        def y_values(piece):
            return staged(piece + Y_LAG)[:, K:].rearrange("p (i n) -> p i n", i=2)

        def widen_x(tile, blocks, on_scalar):
            scales = early_scale[:, tile, :] if tile < EARLY_TILES else late_scale[:, tile - EARLY_TILES, :]
            for j in blocks:
                values = x_values(tile)[:, j * P : (j + 1) * P]
                fp8_values = x_bytes[tile // 2][:, tile % 2, j * P : (j + 1) * P].bitcast(FP8)
                if on_scalar:
                    nc.scalar.activation(out=values, in_=fp8_values, func=ACT.Copy, scale=scales[:, j : j + 1])
                else:
                    nc.vector.tensor_scalar(
                        out=values, in0=fp8_values, scalar1=scales[:, j : j + 1], scalar2=None, op0=ALU.mult
                    )

        def round_window(window, on_gpsimd):
            tile, piece = window + X_LEAD, window - Y_LAG
            has_x, has_y = tile < TILES, piece >= 0
            values = staged(window)[:, (0 if has_x else K) : (2 * K if has_y else K)]
            rounded = work.tile([P, values.shape[1]], BF16, name="rounded", tag="rounded")
            in_order = values.rearrange("p (w u e) -> p u w e", u=2, e=2)
            sorted_out = rounded[:].rearrange("p (u w e) -> p u w e", u=2, e=2)
            if on_gpsimd:
                nc.gpsimd.tensor_scalar(out=sorted_out, in0=in_order, scalar1=1.0, scalar2=1.0, op0=ALU.mult, op1=ALU.mult)
            else:
                nc.vector.tensor_copy(out=sorted_out, in_=in_order)
            runs = rounded[:].bitcast(F32).rearrange("p (u a w) -> p a u w", u=2, w=P)
            if has_x:
                x_words[tile] = runs[:, 0:2, :, :]
            if has_y:
                y_words[piece] = runs[:, 2:4, :, :] if has_x else runs

        def turn_words(name, runs):
            turned = transpose_bank(F32)
            for a in range(2):
                for u in range(2):
                    slot = 2 * a + u
                    nc.tensor.transpose(turned[:, slot * P : (slot + 1) * P], runs[:, a, u, :], ident_f32[:])
            grouped = work.tile([P, K], BF16, name=name, tag=name, align_bytes=64)
            nc.scalar.copy(
                out=grouped[:].bitcast(F32).rearrange("p (a c u) -> p a c u", a=2, u=2),
                in_=turned[:].rearrange("p (a u c) -> p a c u", a=2, u=2),
            )
            return grouped

        x_grouped, x_codes, x_scales = {}, {}, {}

        def turn_x(tile):
            x_grouped[tile] = turn_words("x_grouped", x_words[tile])

        def quantize_x(tile):
            pair, i = divmod(tile, 2)
            if i == 0:
                x_codes[pair] = work.tile([P, HALVES, PAIR], U32, name="x_codes", tag="x_codes", align_bytes=64)
                x_scales[pair] = work.tile([P, HALVES, PAIR], U8, name="x_scales", tag="x_scales", align_bytes=64)
            for half in range(HALVES):
                nc.vector.quantize_mx(
                    out=x_codes[pair][:, half, i * P : (i + 1) * P].bitcast(FP8X4),
                    scales=x_scales[pair][:, half, i * P : (i + 1) * P],
                    in_=x_grouped[tile][:, half * HALF : (half + 1) * HALF],
                )

        u_turned = {}

        def middle(stage):
            pair, quarter = divmod(stage, QUARTERS)
            spans = [(jj, 2 * quarter + jj, slice(jj * PAIR, (jj + 1) * PAIR)) for jj in range(2)]
            product = psum.tile([P, HALF], F32, name="product", tag="product", bufs=2)
            b_turned = transpose_bank(BF16)
            x_turned = transpose_bank(F32)
            for jj, j, cols in spans:
                for half in range(HALVES):
                    nc.tensor.matmul_mx(
                        out=product[:, cols],
                        lhsT=g_codes[half, quarter][:, jj * P : (jj + 1) * P].bitcast(FP8X4),
                        lhsT_scale=g_scales[half, quarter][:, jj * P : (jj + 1) * P],
                        rhs=x_codes[pair][:, half, :].bitcast(FP8X4),
                        rhs_scale=x_scales[pair][:, half, :],
                        start=(half == 0),
                        stop=(half == HALVES - 1),
                    )
            for jj, j, cols in spans:
                for i in range(2):
                    nc.tensor.transpose(
                        b_turned[:, cols][:, i * P : (i + 1) * P], b_rows[pair][:, i, j * P : (j + 1) * P], ident_bf16[:]
                    )
            for jj, j, cols in spans:
                for i in range(2):
                    nc.tensor.transpose(
                        x_turned[:, cols][:, i * P : (i + 1) * P],
                        x_values(2 * pair + i)[:, j * P : (j + 1) * P],
                        ident_f32[:],
                    )
            p_term = work.tile([P, HALF], F32, name="p_term", tag="p_term")
            px_term = work.tile([P, HALF], F32, name="px_term", tag="px_term")
            u_term = work.tile([P, HALF], F32, name="u_term", tag="u_term", bufs=6)
            for jj, j, cols in spans:
                nc.scalar.activation(
                    out=p_term[:, cols], in_=product[:, cols], func=ACT.Copy, scale=neg_step[:, j : j + 1]
                )
            for jj, j, cols in spans:
                nc.vector.scalar_tensor_tensor(
                    out=px_term[:, cols],
                    in0=x_turned[:, cols],
                    scalar=factors[:, CHUNKS + j : CHUNKS + j + 1],
                    in1=p_term[:, cols],
                    op0=ALU.mult,
                    op1=ALU.add,
                )
            for jj, j, cols in spans:
                nc.vector.scalar_tensor_tensor(
                    out=u_term[:, cols],
                    in0=b_turned[:, cols],
                    scalar=factors[:, j : j + 1],
                    in1=px_term[:, cols],
                    op0=ALU.mult,
                    op1=ALU.add,
                )
                u_turned[pair, j] = u_term[:, cols]

        u_rows, above, y_grouped, y_scales = {}, {}, {}, {}

        def turn_back(piece, i):
            pair, half = divmod(piece, HALVES)
            u_rows[piece, i] = transpose_bank(F32)
            for jj in range(HALF // P):
                nc.tensor.transpose(
                    u_rows[piece, i][:, jj * P : (jj + 1) * P],
                    u_turned[pair, half * (HALF // P) + jj][:, i * P : (i + 1) * P],
                    ident_f32[:],
                )
            above[piece, i] = work.tile([P, HALF], F32, name="above", tag="above")
            nc.scalar.activation(out=above[piece, i][:], in_=u_rows[piece, i][:], func=ACT.Relu, bias=-THETA)

        def threshold(piece, i):
            pair, half = divmod(piece, HALVES)
            nc.vector.scalar_tensor_tensor(
                out=y_values(piece)[:, i, :],
                in0=u_rows[piece, i][:],
                scalar=THETA,
                in1=above[piece, i][:],
                op0=ALU.add,
                op1=ALU.min,
            )
            if i == 1:
                nc.sync.dma_start(out=pair_rows(out_0, pair)[:, :, half * HALF : (half + 1) * HALF], in_=y_values(piece))

        def turn_y(piece):
            y_grouped[piece] = turn_words("y_grouped", y_words[piece])

        def quantize_y(piece):
            pair, half = divmod(piece, HALVES)
            batch, place = divmod(pair, SCALE_PAIRS)
            if half == 0 and place == 0:
                y_scales[batch] = work.tile(
                    [P, HALVES, SCALE_PAIRS * PAIR], U8, name="y_scales", tag="y_scales", bufs=2, align_bytes=64
                )
            y_codes = work.tile([P, PAIR], U32, name="y_codes", tag="y_codes", align_bytes=64)
            nc.vector.quantize_mx(
                out=y_codes[:].bitcast(FP8X4),
                scales=y_scales[batch][:, half, place * PAIR : (place + 1) * PAIR],
                in_=y_grouped[piece][:],
            )
            code_rows = out_1[half, :, pair * PAIR : (pair + 1) * PAIR, :].rearrange("p m t -> p (m t)")
            nc.sync.dma_start(out=code_rows.bitcast(I32), in_=y_codes[:].bitcast(I32))
            if half == HALVES - 1 and place == SCALE_PAIRS - 1:
                tokens = slice(batch * SCALE_PAIRS * PAIR, (batch + 1) * SCALE_PAIRS * PAIR)
                scale_planes = out_2[:, :, tokens].bitcast(I32)
                queue = nc.scalar if piece == PIECES - 1 else nc.sync
                for quadrant in range(4):
                    queue.dma_start(
                        out=scale_planes[:, 4 * quadrant : 4 * quadrant + 4, :].rearrange("h r m -> r h m"),
                        in_=y_scales[batch][32 * quadrant : 32 * quadrant + 4, :, :].bitcast(I32),
                    )

        all_blocks = range(CHUNKS)
        widen_x(0, all_blocks, False)
        widen_x(1, all_blocks, True)
        interleave_g(0, 0)
        interleave_g(1, 0)
        round_window(0 - X_LEAD, False)
        round_window(1 - X_LEAD, False)
        turn_x(0)
        turn_x(1)
        quantize_g(0, 0)
        interleave_g(0, 1)
        interleave_g(1, 1)
        quantize_g(1, 0)
        make_factors()
        quantize_x(0)
        quantize_x(1)
        quantize_g(0, 1)
        widen_x(2, all_blocks, False)
        round_window(2 - X_LEAD, False)

        plan = {}

        def at(stage, phase, call, *args):
            plan.setdefault((stage, phase), []).append((call, args))

        at(0, TURN_WORDS, turn_x, 2)
        at(1, QUANTIZE, quantize_x, 2)
        at(0, QUANTIZE, quantize_g, 1, 1)
        for quarter in range(2, QUARTERS):
            at(quarter - 2, INTERLEAVE_VECTOR, interleave_g, 0, quarter)
            at(quarter - 2, INTERLEAVE_SCALAR, interleave_g, 1, quarter)
            for half in range(HALVES):
                at(quarter - 1, QUANTIZE, quantize_g, half, quarter)
        late_stage = 2 * (TILES - X_LEAD)
        for tile in range(3, TILES):
            window = tile - X_LEAD
            stage = max(2 * window, window + 1)
            at(stage - 1, WIDEN_SCALAR, widen_x, tile, range(SCALAR_BLOCKS), True)
            at(stage, WIDEN_VECTOR, widen_x, tile, range(SCALAR_BLOCKS, CHUNKS), False)
            if window > 0:
                at(stage, ROUND_GPSIMD, round_window, window, True)
            else:
                at(stage, ROUND_VECTOR, round_window, window, False)
            at(max(2 * window + 2, stage + 1), TURN_WORDS, turn_x, tile)
            if 2 * window + 4 < late_stage:
                at(2 * window + 4, QUANTIZE, quantize_x, tile)
            else:
                at(2 * window + 3, QUANTIZE_LATE, quantize_x, tile)
        last_window = PIECES - 1 + Y_LAG
        for window in range(TILES - X_LEAD, last_window):
            at(2 * window, ROUND_GPSIMD, round_window, window, True)
        at(2 * last_window, ROUND_LAST, round_window, last_window, False)
        for stage in range(STAGES):
            at(stage, MIDDLE, middle, stage)
        for pair in range(B_BUFS, PAIRS):
            at(QUARTERS * (pair - B_BUFS + 1), MIDDLE, load_b, pair)
        for piece in range(PIECES):
            for i in range(2):
                at(2 * (piece + 1) + i, TURN_BACK, turn_back, piece, i)
                at(2 * (piece + 1) + i, THRESHOLD, threshold, piece, i)
            stage = 2 * (piece + Y_LAG)
            wait = 3 if stage < STAGES else 1
            at(stage + wait, TURN_WORDS, turn_y, piece)
            if late_stage <= stage + wait + 1 < STAGES:
                at(stage + wait + 2, QUANTIZE_LATE, quantize_y, piece)
            else:
                at(stage + wait + 1, QUANTIZE, quantize_y, piece)
        for key in sorted(plan):
            for call, args in plan[key]:
                call(*args)
